import numpy as np, ml_dtypes
CORES = [2,6,10,14,18,22,26,30]
N = 8
import mx_ref
BF = ml_dtypes.bfloat16
def gentries(a):
    return np.ascontiguousarray(a.reshape(8, 16, -1).transpose(0, 2, 1)).reshape(8, -1)
def gtable(e):
    e = np.asarray(e); return np.ascontiguousarray(e.reshape(8, -1, 16).transpose(0, 2, 1)).reshape(128, -1).astype(np.int32)
def gcols(t, e):
    v = np.concatenate([t.reshape(8, 16, -1, 4), np.zeros((8, 16, 1, 4), BF)], axis=2)
    return np.ascontiguousarray(np.stack([v[g][:, e[g]] for g in range(8)])).reshape(128, -1)
def gpick(z, e):
    return np.concatenate([z[16 * g:16 * g + 16][:, e[g]] for g in range(8)])
def tile(rs):
    return np.stack(rs, axis=2).reshape(128, -1).astype(BF)
def pick(q, e):
    c = np.concatenate([q[0].reshape(128, -1, 4), np.zeros((128, 1, 4), np.uint8)], axis=1); s = np.concatenate([q[1], np.ones((16, 1), np.uint8)], axis=1)
    return (np.ascontiguousarray(c[:, e].reshape(128, -1)), np.ascontiguousarray(s[:, e]))
def join(*qs):
    return (np.concatenate([q[0] for q in qs], axis=1), np.concatenate([q[1] for q in qs], axis=1))
def put(q, e, v):
    c, s = q[0].reshape(128, -1, 4).copy(), q[1].copy(); c[:, e] = v[0].reshape(128, -1, 4); s[:, e] = v[1]
    return (c.reshape(128, -1), s)
def pk(c, s):
    return (np.ascontiguousarray(c), mx_ref.live(s))
def emit(q):
    return q[0], q[1]
def packed(v, rng):
    q = [mx_ref.quantize(np.ascontiguousarray(v[r])) for r in range(N)]
    return np.stack([a for a, b in q]), np.stack([mx_ref.plane(b, rng) for a, b in q])
def f(rng, *shape):
    return mx_ref.flush((rng.standard_normal(shape, dtype=np.float32) * np.exp2(rng.integers(-2, 3, shape[:-1] + (1,)))).astype(BF))
def wide(rng, *shape, cols=0):
    v = rng.standard_normal(shape, dtype=np.float32) * np.exp2(rng.integers(-12, 13, shape)).astype(np.float32)
    if cols: v *= np.repeat(np.exp2(rng.integers(-cols, cols + 1, shape[:-2] + (1, shape[-1] // 4))) * (rng.random(shape[:-2] + (1, shape[-1] // 4)) > 0.0625), 4, axis=-1).astype(np.float32)
    return mx_ref.flush(v.astype(BF))
C, R = 256, 3
def big(v):
    v = v.astype(np.float32)
    v[np.abs(v) < np.float32(2.0 ** -16)] = 0
    return v.astype(BF)
def numbers_of(rng):
    return {"x": big(f(rng, N, 128, 4 * C)), "u": np.array(f(rng, N, 128, 512)), "v": np.array(f(rng, N, 128, 512))}
def lookups(e):
    return {"ct": np.stack([gtable(e[r]) for r in range(N)])}
def any_lookups(rng):
    return rng.integers(0, 16, (N, 8, 256))
def layers(rng):
    return big(f(rng, N, 128, 2048)).reshape(N, 8, 16, 4, 8, 16, 4)
def weights(rng, w):
    c, p = packed(np.ascontiguousarray(w).reshape(N, 128, 2048), rng)
    return {"wc": c, "ws": p}
def signs(c):
    return ((c[:, :, None] >> np.arange(3, -1, -1)[:, None]) & 1) * 2.0 - 1.0
def single(d, k):
    u = d["u"].reshape(N, 128, 128, 4)
    for b in range(4):
        u[:, :, b::16] = 0
        for h in range(0, 128, 16): u[:, h + b, h + b, 0] = k
    return u
def setup_inputs(rng):
    return {**numbers_of(rng), **lookups(any_lookups(rng)), **weights(rng, layers(rng))}
def setup_inputs_near(rng):
    d = numbers_of(rng)
    x = d["x"].reshape(N, 8, 16, C, 4)
    o = rng.permutation(N) % 4
    k = np.where(o < 2, 2.0 ** -30, 1.0)
    u = single(d, k.astype(np.float32).astype(BF))
    x[:, :, :8] = 0
    for r in range(N):
        s = rng.integers(-1, 2, (8, 4, C)) * k[r]
        for g in rng.permutation(8)[:4]: s[g, :, rng.integers(C)] = 2.0 ** 29 * rng.choice([-1.0, 1.0], 4)
        two = o[r] in (0, 3)
        x[r, :, :4, :, 0] = (s * (1.125 if two else 1.0)).astype(np.float32).astype(BF)
        if two:
            x[r, :, 4:8, :, 0] = (-s).astype(np.float32).astype(BF)
            for h in range(0, 128, 16):
                for b in range(4):
                    u[r, h + b, h + b, 0] = 1.125 * k[r]
                    u[r, h + 4 + b, h + b, 0] = 1.25 * k[r]
    w = layers(rng)
    w[:, :, :8] = 0
    w[:, :, :, :, :, :8] = 0
    return {"x": x.reshape(N, 128, 4 * C), "u": u.reshape(N, 128, 512), "v": d["v"], **lookups(any_lookups(rng)), **weights(rng, w)}
def setup_inputs_late(rng):
    d = numbers_of(rng)
    x = d["x"].reshape(N, 8, 16, C, 4)
    c = (rng.permutation(N) % 2 * 2.0 - 1.0).astype(np.float32).astype(BF)
    x[:, :, 0] = c[:, None, None, None]
    u = d["u"].reshape(N, 128, 128, 4)
    for b in range(4):
        u[:, :, b::16] = 0
        for h in range(0, 128, 16): u[:, h, h + b, b] = 1
    return {"x": x.reshape(N, 128, 4 * C), "u": u.reshape(N, 128, 512), "v": d["v"], **lookups(any_lookups(rng)), **weights(rng, layers(rng))}
def setup_inputs_one(rng):
    d = numbers_of(rng)
    x = d["x"].reshape(N, 8, 16, C, 4)
    c, e, n = rng.integers(0, 16, (N, 8, C)), any_lookups(rng), np.arange(256)
    for r in rng.permutation(N)[:N // 2]:
        a = (rng.integers(C) - np.arange(C)) % C
        h = np.arange(8)[:, None] % 2
        c[r] = np.where(a < 256, np.where(h == 0, a // 16, a % 16), c[r])
        e[r] = np.where(h == 0, n // 16, n % 16)
        e[r, 7] = n // 16
    x[:, :, :8] = 0
    x[:, :, :4, :, 0] = signs(c).astype(np.float32).astype(BF)
    u = single(d, np.ones(N, np.float32).astype(BF))
    w = layers(rng)
    w[:, :, :, :, :, :8] = 0
    return {"x": x.reshape(N, 128, 4 * C), "u": u.reshape(N, 128, 512), "v": d["v"], **lookups(e), **weights(rng, w)}
def setup_inputs_ends(rng):
    d = numbers_of(rng)
    o = rng.permutation(N) % 4
    u = single(d, np.where(o == 1, 2.0 ** -30, 2.0 ** 30).astype(np.float32).astype(BF))
    x = 2.0 ** 30 * (0.75 + 0.1 * rng.random((N, 8, 16, C, 4))) * rng.choice([-1.0, 1.0], (N, 8, 1, C, 1))
    x[:, :, :8] = 0
    x[:, :, :4, :, 0] = signs(rng.integers(0, 16, (N, 8, C))) * 2.0 ** 30
    e = rng.integers(0, 2, (N, 8, 256)) * 15
    w = np.zeros((N, 128, 4, 128, 4), np.float32)
    i = np.arange(128)
    i = i[i % 16 >= 8]
    for r in range(N):
        if o[r] == 0:
            x[r] = 2.0 ** 30 * rng.choice([-1.0, 1.0], (1, 1, C, 1))
            for b in range(4): u[r][:, b::16] = (2.0 ** 30 * rng.choice([-1.0, 1.0], (1, 8, 1)) * np.ones((128, 1, 4))).astype(np.float32).astype(BF)
            e[r] = 15
        if o[r] == 1:
            x[r, :, :4] *= 2.0 ** -60
            x[r, :, 8:] = 2.0 ** -30 * rng.choice([-1.0, 1.0], (8, 8, C, 4))
            e[r] = 0
        if o[r] == 2: x[r, :, :8] = 0
        if o[r] == 3: e[r] = rng.integers(0, 2, (8, 1)) * 15
        if o[r] >= 2:
            for b in range(4): w[r, i, b, i, b] = rng.choice([-1.0, 1.0], len(i))
    d["v"] = (np.where(d["v"] < 0, -1.0, 1.0) * np.where(rng.permutation(N) % 2, 2.0 ** -30, 2.0 ** 30)[:, None, None]).astype(np.float32).astype(BF)
    return {"x": x.astype(np.float32).reshape(N, 128, 4 * C).astype(BF), "u": u.reshape(N, 128, 512), "v": d["v"], **lookups(e), **weights(rng, w.astype(BF))}
def setup_inputs_spread(rng):
    d = setup_inputs(rng)
    d["x"] = big(wide(rng, N, 128, 4 * C, cols=6))
    return d
def check_inputs(d):
    b = []
    for k in ("x", "u", "v"):
        a = np.abs(d[k].astype(np.float32))
        if not (np.isfinite(a).all() and ((a == 0) | (a >= 2.0 ** -30) & (a <= 2.0 ** 30)).all()): b.append("a value of " + k)
    if not ((d["ct"] >= 0) & (d["ct"] < 16)).all(): b.append("an entry of ct")
    none, least, most = [emit(mx_ref.quantize(np.full((128, 16), k, np.float32).astype(BF)))[1][0, 0] for k in (0.0, 2.0 ** -30, 2.0 ** 30)]
    for r in range(N):
        if ((d["wc"][r] == 0x7F) | (d["wc"][r] == 0xFF)).any(): b.append("wc: a code that is no number")
        s = mx_ref.live(d["ws"][r])
        if ((s != none) & ((s < least) | (s > most))).any(): b.append("ws: a scale out of range")
    return b
def reference(x, u, v, ct, wc, ws):
    qu = [mx_ref.quantize(u[r]) for r in range(N)]
    lay = [pk(wc[r], ws[r]) for r in range(N)]
    now = [x[r] for r in range(N)]
    k = [gentries(ct[r]) for r in range(N)]
    for t in range(R):
        place, z = [], []
        for r in range(N):
            s = (mx_ref.matmul(qu[r], mx_ref.quantize(now[r])) > 0).astype(np.int64)
            c = 8 * s[::16] + 4 * s[1::16] + 2 * s[2::16] + s[3::16]
            a = np.zeros((8, C), np.int64)
            a[:4] = 16 * c[::2] + c[1::2]
            a[4] = 16 * k[r][0][a[0]] + k[r][1][a[1]]
            a[5] = 16 * k[r][2][a[2]] + k[r][3][a[3]]
            a[6] = 16 * k[r][4][a[4]] + k[r][5][a[5]]
            a[7] = 16 * k[r][6][a[6]] + k[r][7][16 * c[7] + c[0]]
            place.append((a + np.arange(C)) % C)
            z.append(mx_ref.quantize(gcols(now[r], place[r])))
        made = []
        for r in range(N):
            q, e = z[(r - 1 - t) % N], place[r][[1, 0, 3, 2, 5, 4, 7, 6]]
            made.append(tile([gpick(mx_ref.matmul(pick(lay[r], np.arange(128 * b, 128 * b + 128)), q) * np.float32(0.03125), e) + now[r][:, b::4].astype(np.float32) for b in range(4)]))
        now = made
    y, lo = np.zeros((N, 128, C), np.float32), np.zeros((N, 8, C), np.float32)
    oc, osc = np.zeros((N, 128, 4 * C), np.uint8), np.zeros((N, 16, C), np.uint8)
    for r in range(N):
        q = mx_ref.quantize(now[r])
        y[r] = mx_ref.matmul(mx_ref.quantize(v[r]), q)
        lo[r] = place[r]
        oc[r], osc[r] = emit(q)
    return {"y": y, "lo": lo, "oc": oc, "osc": osc}

@@ -1,0 +1,326 @@
+from concourse.mybir import dt, AluOpType, ActivationFunctionType
+
+C = 256
+R = 3
+X4 = "float8_e4m3fn_x4"
+SCRATCH = {
+    "ut": ("sbuf", [128, 512], "bfloat16"), "vt": ("sbuf", [128, 512], "bfloat16"),
+    "qu": ("sbuf", [128, 128], X4), "su": ("sbuf", [128, 128], "uint8"),
+    "qup": ("sbuf", [128, 128], X4), "sup": ("sbuf", [128, 128], "uint8"),
+    "qv": ("sbuf", [128, 128], X4), "sv": ("sbuf", [128, 128], "uint8"),
+    "wq": ("sbuf", [128, 512], X4), "wp": ("sbuf", [128, 512], "uint8"),
+    "ps": ("psum", [128, 4096], "float32"),
+    "raw": ("sbuf", [128, 512], "int32"), "wt": ("sbuf", [128, 768], "bfloat16"),
+    "kk": ("sbuf", [128, 192], "float32"), "kt": ("sbuf", [128, 192], "float32"),
+    "p16": ("sbuf", [128, 8], "float32"),
+    "uci": ("sbuf", [128, 8], "int32"), "ucm": ("sbuf", [128, 8], "int32"), "ucl": ("sbuf", [128, 8], "uint16"),
+    "swl": ("sbuf", [128, 16], "uint16"), "jj": ("sbuf", [128, 16], "float32"),
+    "dd": ("sbuf", [128, 128], "bfloat16"),
+    "bits": ("sbuf", [128, 256], "bfloat16"), "bt": ("sbuf", [128, 256], "bfloat16"), "sc": ("sbuf", [128, 256], "bfloat16"),
+    "l1": ("sbuf", [128, 16], "uint16"), "l2": ("sbuf", [128, 16], "uint16"), "l3": ("sbuf", [128, 16], "uint16"),
+    "f1": ("sbuf", [128, 256], "bfloat16"), "f2": ("sbuf", [128, 256], "bfloat16"), "f3": ("sbuf", [128, 256], "bfloat16"),
+    "t1": ("sbuf", [128, 256], "bfloat16"), "t2": ("sbuf", [128, 256], "bfloat16"), "t3": ("sbuf", [128, 256], "bfloat16"),
+    "aa": ("sbuf", [128, 16], "float32"), "a6": ("sbuf", [128, 8], "float32"), "ee": ("sbuf", [128, 16], "float32"),
+    "a1": ("sbuf", [128, 16], "float32"), "lz": ("sbuf", [128, 64], "uint16"),
+    "ge": ("sbuf", [128, 16], "float32"), "tin": ("sbuf", [128, 32], "bfloat16"),
+    "y1": ("sbuf", [128, 32], "bfloat16"), "y2": ("sbuf", [128, 32], "bfloat16"), "y3": ("sbuf", [128, 32], "bfloat16"),
+    "lsib": ("sbuf", [128, 16], "uint16"), "lown": ("sbuf", [128, 16], "uint16"),
+    "lof": ("sbuf", [128, 256], "float32"),
+    "hh": ("sbuf", [128, 1024], "float32"), "yo": ("sbuf", [128, 256], "float32"),
+}
+for _t in range(R + 1):
+    SCRATCH["xs%d" % _t] = ("sbuf", [128, 2048 if _t < R else 1024], "bfloat16")
+    SCRATCH["qx%d" % _t] = ("sbuf", [128, C], X4)
+    SCRATCH["sx%d" % _t] = ("sbuf", [128, C], "uint8")
+for _t in range(R):
+    SCRATCH["zz%d" % _t] = ("sbuf", [128, 1024], "bfloat16")
+    SCRATCH["qz%d" % _t] = ("sbuf", [128, C], X4)
+    SCRATCH["sz%d" % _t] = ("sbuf", [128, C], "uint8")
+    SCRATCH["lq%d" % _t] = ("sbuf", [128, C], X4)
+    SCRATCH["ls%d" % _t] = ("sbuf", [128, C], "uint8")
+
+NDMA = 32
+NCALL = 3
+SEMAPHORES = ["cv", "cs", "cp", "cg", "sent"] + ["arr%d" % _t for _t in range(R)] + ["d%d" % _i for _i in range(NDMA)]
+
+A = AluOpType
+COPY = ActivationFunctionType.Copy
+
+
+def rank_program(g, core, T, topo):
+    rank = T.rank_of(core)
+    if rank is None:
+        return
+    cores = T.cores
+    n = len(cores)
+
+    Q = {"v": g.vector, "s": g.scalar, "p": g.tensor, "g": g, "y": g.sync}
+    csem = {"v": "cv", "s": "cs", "p": "cp", "g": "cg"}
+    count = {}
+    known = {q: {} for q in Q}
+    wrote, readers = {}, {}
+    ndma = [0]
+
+    def wait(q, tok):
+        sem, c, snap = tok
+        k = known[q]
+        if k.get(sem, 0) >= c:
+            return
+        Q[q].wait_ge(T.sem[sem], c)
+        k[sem] = c
+        for s2, c2 in snap.items():
+            if k.get(s2, 0) < c2:
+                k[s2] = c2
+
+    def run(q, fn, rd, wr, dma=False):
+        deps = []
+        for key in rd:
+            if key in wrote:
+                deps.append(wrote[key])
+        for key in wr:
+            if key in wrote:
+                deps.append(wrote[key])
+            deps.extend(readers.get(key, []))
+        deps.sort(key=lambda tk: -tk[1])
+        for tk in deps:
+            wait(q, tk)
+        if dma:
+            sem, inc = "d%d" % ndma[0], 16
+            ndma[0] += 1
+        else:
+            sem, inc = csem[q], 1
+        fn().then_inc(T.sem[sem], inc)
+        count[sem] = count.get(sem, 0) + inc
+        tok = (sem, count[sem], dict(known[q]))
+        for key in rd:
+            readers.setdefault(key, []).append(tok)
+        for key in wr:
+            wrote[key] = tok
+            readers[key] = []
+        return tok
+
+    V, S, P = g.vector, g.scalar, g.tensor
+
+    def v(fn, rd, wr):
+        return run("v", fn, rd, wr)
+
+    def s(fn, rd, wr):
+        return run("s", fn, rd, wr)
+
+    def dma(q, out, in_, rd, wr):
+        return run(q, lambda: Q[q].dma_start(out, in_), rd, wr, dma=True)
+
+    def u8(ap):
+        return ap.bitcast(dt.uint8)
+
+    def u32(ap):
+        return ap.bitcast(dt.uint32)
+
+    def bank(b, w):
+        return T.ps[:, 512 * b:512 * b + w]
+
+    def engines_of(r):
+        m = -1
+        for t in range(R):
+            m &= topo.mask(cores[r], cores[(r + 1 + t) % n])
+        return m
+
+    def ones(m):
+        return bin(m).count("1")
+
+    X = [T["xs%d" % t] for t in range(R + 1)]
+    xk = lambda t: [("x", t, b) for b in range(4)]
+    xdk = lambda t: [("xd", t, b) for b in range(4)]
+
+    dma("y", T.ut[:], T.u[:], [], ["ut"])
+    dma("s", X[0][:, 0:512], T.x[:, 0:512], [], ["x0h0"])
+    dma("y", X[0][:, 512:1024], T.x[:, 512:1024], [], ["x0h1"])
+    v(lambda: V.memset(T.raw[64:128, 0:256], 0), [], ["rawA"])
+    v(lambda: V.memset(T.raw[64:128, 256:512], 0), [], ["rawB"])
+    run("g", lambda: g.iota(T.kk[:, 128:160], [[0, 2], [1, 16]], 0, 0, allow_small_or_imprecise_dtypes=True), [], ["k4"])
+    for h in range(2):
+        run("g", lambda: g.iota(T.kk[:, 160 + 16 * h:176 + 16 * h], [[112, 2], [16, 2], [1, 4]], 0, 0,
+                                allow_small_or_imprecise_dtypes=True), [], [("k5", h)])
+    run("g", lambda: g.iota(T.raw[0:64, :], [[0, 2], [1, 16], [16, 16]], 0, 0), [], ["rawI"])
+    run("g", lambda: g.iota(T.wt[:, 512:768], [[1, 256]], 0, 0, allow_small_or_imprecise_dtypes=True), [], ["wtI"])
+    pieces = [("s", 64, 0, 0, 6), ("y", 80, 0, 0, 6), ("s", 96, 0, 0, 1), ("y", 112, 0, 0, 1),
+              ("s", 65, 1, 3, 1), ("y", 81, 1, 3, 1), ("s", 96, 1, 2, 6), ("y", 112, 1, 2, 6)]
+    rawk = [[], []]
+    for i, (q, p0, h, t0, nt) in enumerate(pieces):
+        dma(q, T.raw[p0:p0 + nt, 256 * h:256 * h + 256], T.ct[16 * t0:16 * (t0 + nt), :], ["rawA" if h == 0 else "rawB"], [("raw", i)])
+        rawk[h].append(("raw", i))
+    dma("y", X[0][:, 1024:2048], T.x[:], [], xdk(0))
+    dma("y", u8(T.wq[:]), T.wc[:], [], ["wq"])
+    dma("y", T.wp[:], T.ws[:], [], ["wp"])
+    dma("y", T.vt[:], T.v[:], [], ["vt"])
+
+    v(lambda: V.memset(T.kk[:, 0:96], 0.0), [], ["k0"])
+    v(lambda: V.memset(T.kk[:, 96:128], 1.0), [], ["k3"])
+    v(lambda: V.memset(T.kk[:, 8:16], 1e29), ["k0"], ["k0a"])
+    v(lambda: V.memset(T.kk[:, 32:48:8], -2.0), ["k0"], ["k0b"])
+    v(lambda: V.memset(T.kk[:, 64:72], 32.0), ["k0"], ["k0c"])
+    v(lambda: V.memset(T.kk[:, 80:88], 32.0), ["k0"], ["k0d"])
+    v(lambda: V.memset(T.kk[:, 96:128:4], 16.0), [], ["k3"])
+    v(lambda: V.memset(T.dd[:], 2.0), [], ["dd"])
+    v(lambda: V.transpose(T.kt[:], T.kk[:]), ["k0", "k0a", "k0b", "k0c", "k0d", "k3", "k4", ("k5", 0), ("k5", 1)], ["kt"])
+    v(lambda: V.memset(T.dd[:, 0:128:8], 0.0), [], ["dd"])
+    thr, add0, lo32, scl, p15, gu = [T.kt[:, 32 * i:32 * i + 1] for i in range(6)]
+    Rw = lambda a, b, c=1: T.kk[:, 128 + a:128 + b:c]
+    for i, (a, b, src) in enumerate([(0, 4, Rw(0, 4)), (4, 6, Rw(1, 4, 2)), (6, 8, Rw(0, 4, 2))]):
+        v(lambda: V.tensor_scalar(T.uci[:, a:b], src, lo32, gu, A.mult, A.add), ["kt"], [("uci", i)])
+    v(lambda: V.tensor_scalar(T.p16[:, 0:1], p15, 16.0, None, A.mult), ["kt"], ["p16"])
+    v(lambda: V.tensor_scalar(T.ucm[:], T.uci[:], 127, None, A.bitwise_and), [("uci", i) for i in range(3)], ["ucm"])
+    v(lambda: V.tensor_scalar(T.swl[:], Rw(0, 16), T.p16[:, 0:1], None, A.add), ["p16"], ["swl"])
+    v(lambda: V.tensor_copy(T.ucl[:], T.ucm[:]), ["ucm"], ["ucl"])
+
+    v(lambda: V.quantize_mx(T.qu[:], T.su[:], T.ut[:]), ["ut"], ["qu"])
+    v(lambda: V.tensor_scalar(T.jj[:], Rw(0, 16), 16.0, p15, A.mult, A.add), ["kt"], ["jj"])
+    v(lambda: V.tensor_copy(u32(T.qup[:]), u32(T.qu[:]).indirect(T.ucl[:, 0:8])), ["qu", "ucl"], ["qup"])
+    s(lambda: S.activation(T.sup[:], T.su[:].indirect(T.ucl[:, 0:8]), COPY), ["qu", "ucl"], ["sup"])
+
+    def table(h):
+        v(lambda: V.tensor_scalar(T.wt[:, 256 * h:256 * h + 256], T.raw[:, 256 * h:256 * h + 256].indirect(T.swl[:]), scl, None, A.mult),
+          rawk[h] + ["rawI", "swl", "kt"], [("wt", h)])
+
+    def quant_x(t):
+        for h in range(2):
+            v(lambda: V.quantize_mx(T["qx%d" % t][:, 128 * h:128 * h + 128], T["sx%d" % t][:, 128 * h:128 * h + 128],
+                                    X[t][:, 512 * h:512 * h + 512]),
+              ["x0h%d" % h] if t == 0 else xk(t), [("qx", t, h)])
+
+    def product(stat, scale, keys, t):
+        for h in range(2):
+            run("p", lambda: P.matmul_mx(bank(5 + h, 128), stat, scale, T["qx%d" % t][:, 128 * h:128 * h + 128],
+                                         T["sx%d" % t][:, 128 * h:128 * h + 128], True, True),
+                keys + [("qx", t, h)], [("ps", 5 + h)])
+
+    def lookup(lst, lk, win, wk, f, fk, tt, tk, between):
+        v(lambda: V.tensor_copy(f[:, 0:128], win.indirect(lst[:, 0:8])), lk + wk, [(fk, 0)])
+        s(lambda: S.activation(f[:, 128:256], win.indirect(lst[:, 8:16]), COPY), lk + wk, [(fk, 1)])
+        between()
+        v(lambda: V.transpose(tt[:], f[:]), [(fk, 0), (fk, 1)], [tk])
+
+    mymask = engines_of(rank)
+    sent = 0
+    win12, win3, winI = T.wt[:, 0:512], T.wt[:, 256:768], T.wt[:, 512:768]
+    w12, w3 = [("wt", 0), ("wt", 1)], [("wt", 1), "wtI"]
+
+    for t in range(R):
+        quant_x(t)
+        product(T.qup[:], T.sup[:], ["qup", "sup"], t)
+        if t == 0:
+            table(0)
+        for h in range(2):
+            v(lambda: V.tensor_scalar(T.bits[:, 128 * h:128 * h + 128], bank(5 + h, 128), thr, add0, A.is_gt, A.add),
+              ["kt"], [("ps", 5 + h), ("bits", h)])
+        for h in range(2):
+            v(lambda: V.transpose(T.bt[:, 128 * h:128 * h + 128], T.bits[:, 128 * h:128 * h + 128]), [("bits", h)], [("bt", h)])
+        for h in range(2):
+            v(lambda: V.tensor_tensor_scan(T.sc[:, 128 * h:128 * h + 128], T.dd[:], T.bt[:, 128 * h:128 * h + 128], 0.0, A.mult, A.add),
+              [("bt", h), "dd"], [("sc", h)])
+        if t == 0:
+            table(1)
+        sck = [("sc", 0), ("sc", 1)]
+        v(lambda: V.tensor_scalar(T.l1[:], T.sc[:, 7:256:16], 256.0, None, A.add), sck, ["l1", "l3a", "l3b"])
+
+        def b1():
+            v(lambda: V.tensor_scalar(T.l2[:], T.sc[:, 15:256:16], 256.0, None, A.add), sck, ["l2"])
+        lookup(T.l1, ["l1", "l3a", "l3b"], win12, w12, T.f1, "f1", T.t1, "t1", b1)
+        v(lambda: V.tensor_tensor(T.t1[64:96, 1:256:16], T.t1[64:96, 1:256:16], T.t1[96:128, 0:256:16], A.add), [], ["t1"])
+        v(lambda: V.tensor_copy(T.l2[64:96, :], T.t1[64:96, 1:256:16]), ["t1"], ["l2"])
+
+        def b2():
+            v(lambda: V.tensor_tensor(T.a1[0:96, :], T.t1[0:96, 1:256:16], T.jj[0:96, :], A.add), ["t1", "jj"], ["a1a"])
+        lookup(T.l2, ["l2"], win12, w12, T.f2, "f2", T.t2, "t2", b2)
+        v(lambda: V.tensor_tensor(T.a6[96:128, :], T.t2[64:96, 4:256:32], T.t2[64:96, 21:256:32], A.add), ["t2"], ["a6"])
+        v(lambda: V.tensor_tensor(T.ee[96:128, :], T.t2[96:128, 5:256:16], T.jj[96:128, :], A.add), ["t2", "jj"], ["ee"])
+        v(lambda: V.tensor_scalar(T.l1[96:128, 0:16:2], T.a6[96:128, :], 256.0, None, A.add), ["a6"], ["l3a"])
+        v(lambda: V.tensor_copy(T.l1[96:128, 1:16:2], T.a6[96:128, :]), ["a6"], ["l3b"])
+        lookup(T.l1, ["l1", "l3a", "l3b"], win3, w3, T.f3, "f3", T.t3, "t3", lambda: None)
+        v(lambda: V.tensor_tensor(T.a1[96:128, :], T.t3[96:128, 4:256:16], T.ee[96:128, :], A.add), ["t3", "ee"], ["a1c"])
+        a1k = ["a1a", "a1c"]
+
+        Z, qz, sz = T["zz%d" % t], T["qz%d" % t], T["sz%d" % t]
+        lq, ls = T["lq%d" % t], T["ls%d" % t]
+        xw = (["x0h0", "x0h1"] if t == 0 else xk(t)) + xdk(t)
+        rid, pid, _ = topo.addr(cores[(rank + 1 + t) % n])
+
+        def zpick(q, e, h):
+            out = Z[:, 512 * h + e:512 * h + 512:4]
+            src = X[t][:].indirect(T.lz[:, 16 * e + 8 * h:16 * e + 8 * h + 8])
+            fn = (lambda: V.tensor_copy(out, src)) if q == "v" else (lambda: S.activation(out, src, COPY))
+            run(q, fn, xw + [("lz", e)], [("z", t, e, h)])
+
+        def zquant(h):
+            return v(lambda: V.quantize_mx(qz[:, 128 * h:128 * h + 128], sz[:, 128 * h:128 * h + 128], Z[:, 512 * h:512 * h + 512]),
+                     [("z", t, e, h) for e in range(4)], [("qz", t, h)])
+
+        def send(dst, src):
+            g.remote_dma(dst, src, T.sem["arr%d" % t], T.sem.sent, pid, rid, mymask)
+
+        for e in (2, 3, 0, 1):
+            v(lambda: V.tensor_scalar(T.lz[:, 16 * e:16 * e + 16], T.a1[:], 4.0, float(e), A.mult, A.add), a1k, [("lz", e)])
+        for e, h in ((2, 0), (3, 0), (2, 1), (3, 1), (1, 1)):
+            zpick("s", e, h)
+        zpick("v", 0, 0)
+        zpick("v", 1, 0)
+        v(lambda: V.tensor_scalar(T.tin[:, 16:32], T.a1[:], 256.0, -256.0, A.is_ge, A.mult), a1k, ["ge"])
+        wait("g", zquant(0))
+        send(u8(lq[:, 0:128]), u8(qz[:, 0:128]))
+        zpick("v", 0, 1)
+        wait("g", zquant(1))
+        send(u8(lq[:, 128:256]), u8(qz[:, 128:256]))
+        send(ls[:], sz[:])
+        sent += NCALL * ones(mymask)
+
+        v(lambda: V.tensor_tensor(T.tin[:, 0:16], T.a1[:], T.tin[:, 16:32], A.add), a1k + ["ge"], ["tin"])
+        v(lambda: V.transpose(T.y1[:], T.tin[:]), ["tin", "ge"], ["y1"])
+        v(lambda: V.tensor_copy(T.y2[:, 0:16], T.y1[:, 16:32]), ["y1"], ["y2a"])
+        v(lambda: V.tensor_copy(T.y2[:, 16:32], T.y1[:, 0:16]), ["y1"], ["y2b"])
+        v(lambda: V.transpose(T.y3[:], T.y2[:]), ["y2a", "y2b"], ["y3"])
+        v(lambda: V.tensor_copy(T.lsib[:], T.y3[:, 0:16]), ["y3"], ["lsib"])
+        if t == 0:
+            v(lambda: V.quantize_mx(T.qv[:], T.sv[:], T.vt[:]), ["vt"], ["qv"])
+        if t == R - 1:
+            v(lambda: V.tensor_copy(T.lown[:], T.tin[:, 0:16]), ["tin"], ["lown"])
+            s(lambda: S.activation(T.lof[:], winI.indirect(T.lown[:]), COPY), ["lown", "wtI"], ["lof"])
+            dma("y", T.lo[:], T.lof[0:128:16, :], ["lof"], ["lo"])
+
+        got = NCALL * ones(engines_of((rank - 1 - t) % n))
+        count["arr%d" % t] = got
+        wait("p", ("arr%d" % t, got, {}))
+        jobs = [(0, 0, 0, 128), (1, 0, 128, 128), (2, 1, 0, 256), (3, 2, 0, 256), (4, 3, 0, 256)]
+        for bk, b, c0, w in jobs:
+            run("p", lambda: P.matmul_mx(bank(bk, w), T.wq[:, 128 * b:128 * b + 128], T.wp[:, 128 * b:128 * b + 128],
+                                         lq[:, c0:c0 + w], ls[:, c0:c0 + w], True, True), ["wq", "wp"], [("ps", bk)])
+        for bk, b, c0, w in jobs:
+            out = T.hh[:, 256 * b + c0:256 * b + c0 + w]
+            if bk == 0:
+                v(lambda: V.tensor_scalar(out, bank(bk, w), 0.03125, None, A.mult), [], [("ps", bk), ("h", bk)])
+            else:
+                s(lambda: S.activation(out, bank(bk, w), COPY, scale=0.03125), [], [("ps", bk), ("h", bk)])
+        for b in range(4):
+            hk = [("h", 0), ("h", 1)] if b == 0 else [("h", b + 1)]
+            v(lambda: V.tensor_tensor(X[t + 1][:, b:1024:4], T.hh[:, 256 * b:256 * b + 256].indirect(T.lsib[:]), X[t][:, b:1024:4], A.add),
+              hk + ["lsib"] + (["x0h0", "x0h1"] if t == 0 else [("x", t, b)]), [("x", t + 1, b)])
+            if t + 1 < R:
+                s(lambda: S.activation(X[t + 1][:, 1024 + b:2048:4], X[t + 1][:, b:1024:4], COPY), [("x", t + 1, b)], [("xd", t + 1, b)])
+
+    quant_x(R)
+    product(T.qv[:], T.sv[:], ["qv"], R)
+    qk = [("qx", R, 0), ("qx", R, 1)]
+    qx, sx = T["qx%d" % R], T["sx%d" % R]
+    dma("y", T.oc[:], u8(qx[:]), qk, ["oc"])
+    v(lambda: V.tensor_copy(T.yo[:, 0:128], bank(5, 128)), [], [("ps", 5), "yo0"])
+    v(lambda: V.tensor_copy(T.yo[:, 128:256], bank(6, 128)), [], [("ps", 6), "yo1"])
+    dma("s", T.osc[4:8, :], sx[32:36, :], qk, [("osc", 1)])
+    dma("s", T.osc[12:16, :], sx[96:100, :], qk, [("osc", 3)])
+    dma("y", T.osc[0:4, :], sx[0:4, :], qk, [("osc", 0)])
+    dma("s", T.y[:, 0:128], T.yo[:, 0:128], ["yo0"], ["y0"])
+    dma("y", T.y[:, 128:256], T.yo[:, 128:256], ["yo1"], ["y1o"])
+    dma("s", T.osc[8:12, :], sx[64:68, :], qk, [("osc", 2)])
+
+    count["sent"] = sent
+    for sem in sorted(count, key=lambda k: (k[0] == "d", len(k), k)):
+        if not any(known[q].get(sem, 0) >= count[sem] for q in Q):
+            wait("g", (sem, count[sem], {}))

@@ -1,8 +1,10 @@
 from concourse.mybir import dt, AluOpType, ActivationFunctionType
 
 C = 256
+H = C // 2
 R = 3
 X4 = "float8_e4m3fn_x4"
+TINY = 1e-35
 SCRATCH = {
     "ut": ("sbuf", [128, 512], "bfloat16"), "vt": ("sbuf", [128, 512], "bfloat16"),
     "qu": ("sbuf", [128, 128], X4), "su": ("sbuf", [128, 128], "uint8"),
@@ -10,22 +12,23 @@ SCRATCH = {
     "qv": ("sbuf", [128, 128], X4), "sv": ("sbuf", [128, 128], "uint8"),
     "wq": ("sbuf", [128, 512], X4), "wp": ("sbuf", [128, 512], "uint8"),
     "ps": ("psum", [128, 4096], "float32"),
-    "raw": ("sbuf", [128, 512], "int32"), "wt": ("sbuf", [128, 768], "bfloat16"),
-    "kk": ("sbuf", [128, 192], "float32"), "kt": ("sbuf", [128, 192], "float32"),
-    "p16": ("sbuf", [128, 8], "float32"),
-    "uci": ("sbuf", [128, 8], "int32"), "ucm": ("sbuf", [128, 8], "int32"), "ucl": ("sbuf", [128, 8], "uint16"),
-    "swl": ("sbuf", [128, 16], "uint16"), "jj": ("sbuf", [128, 16], "float32"),
-    "dd": ("sbuf", [128, 128], "bfloat16"),
+    "kk": ("sbuf", [128, 224], "float32"), "kt": ("sbuf", [128, 224], "float32"), "row": ("sbuf", [128, 32], "float32"),
+    "col": ("sbuf", [128, 256], "bfloat16"), "one": ("sbuf", [128, 24], "float32"), "ucl": ("sbuf", [128, 8], "uint16"),
+    "raw": ("sbuf", [128, 16], "int32"), "tn": ("sbuf", [128, 32], "bfloat16"), "ty": ("sbuf", [128, 48], "bfloat16"),
+    "tz": ("sbuf", [128, 64], "bfloat16"), "lt": ("sbuf", [128, 80], "uint16"),
+    "k0": ("sbuf", [128, 256], "bfloat16"), "k1": ("sbuf", [128, 256], "bfloat16"), "km": ("sbuf", [128, 16], "bfloat16"),
+    "wd": ("sbuf", [128, 512], "bfloat16"), "wm": ("sbuf", [128, 512], "bfloat16"), "wb": ("sbuf", [128, 512], "bfloat16"),
+    "wj": ("sbuf", [128, 288], "bfloat16"), "dd": ("sbuf", [128, 128], "bfloat16"),
     "bits": ("sbuf", [128, 256], "bfloat16"), "bt": ("sbuf", [128, 256], "bfloat16"), "sc": ("sbuf", [128, 256], "bfloat16"),
-    "l1": ("sbuf", [128, 16], "uint16"), "l2": ("sbuf", [128, 16], "uint16"), "l3": ("sbuf", [128, 16], "uint16"),
-    "f1": ("sbuf", [128, 256], "bfloat16"), "f2": ("sbuf", [128, 256], "bfloat16"), "f3": ("sbuf", [128, 256], "bfloat16"),
-    "t1": ("sbuf", [128, 256], "bfloat16"), "t2": ("sbuf", [128, 256], "bfloat16"), "t3": ("sbuf", [128, 256], "bfloat16"),
-    "aa": ("sbuf", [128, 16], "float32"), "a6": ("sbuf", [128, 8], "float32"), "ee": ("sbuf", [128, 16], "float32"),
-    "a1": ("sbuf", [128, 16], "float32"), "lz": ("sbuf", [128, 64], "uint16"),
-    "ge": ("sbuf", [128, 16], "float32"), "tin": ("sbuf", [128, 32], "bfloat16"),
-    "y1": ("sbuf", [128, 32], "bfloat16"), "y2": ("sbuf", [128, 32], "bfloat16"), "y3": ("sbuf", [128, 32], "bfloat16"),
-    "lsib": ("sbuf", [128, 16], "uint16"), "lown": ("sbuf", [128, 16], "uint16"),
-    "lof": ("sbuf", [128, 256], "float32"),
+    "ld": ("sbuf", [128, 16], "uint16"), "lm": ("sbuf", [128, 16], "uint16"), "l3": ("sbuf", [128, 16], "uint16"),
+    "l7": ("sbuf", [128, 16], "uint16"),
+    "fd": ("sbuf", [128, 256], "bfloat16"), "fm": ("sbuf", [128, 256], "bfloat16"), "f3": ("sbuf", [128, 256], "bfloat16"),
+    "td": ("sbuf", [128, 256], "bfloat16"), "tm": ("sbuf", [128, 256], "bfloat16"), "t3": ("sbuf", [128, 256], "bfloat16"),
+    "f7": ("sbuf", [128, 256], "bfloat16"), "s2": ("sbuf", [128, 256], "bfloat16"),
+    "lz": ("sbuf", [128, 64], "uint16"), "wi": ("sbuf", [128, 16], "int32"), "wa": ("sbuf", [128, 64], "int32"),
+    "tin": ("sbuf", [128, 64], "bfloat16"), "y1": ("sbuf", [128, 64], "bfloat16"),
+    "y2": ("sbuf", [128, 32], "bfloat16"), "y3": ("sbuf", [128, 32], "bfloat16"),
+    "lsib": ("sbuf", [128, 16], "uint16"), "lown": ("sbuf", [128, 16], "uint16"), "lof": ("sbuf", [128, 256], "float32"),
     "hh": ("sbuf", [128, 1024], "float32"), "yo": ("sbuf", [128, 256], "float32"),
 }
 for _t in range(R + 1):
@@ -39,12 +42,50 @@ for _t in range(R):
     SCRATCH["lq%d" % _t] = ("sbuf", [128, C], X4)
     SCRATCH["ls%d" % _t] = ("sbuf", [128, C], "uint8")
 
-NDMA = 32
-NCALL = 3
-SEMAPHORES = ["cv", "cs", "cp", "cg", "sent"] + ["arr%d" % _t for _t in range(R)] + ["d%d" % _i for _i in range(NDMA)]
+NDMA = 30
+NCALL = 2
+SEMAPHORES = (["cv", "cs", "cp", "cg", "sent"] + ["arr%d%d" % (_t, _h) for _t in range(R) for _h in range(2)]
+              + ["d%d" % _i for _i in range(NDMA)])
 
 A = AluOpType
-COPY = ActivationFunctionType.Copy
+F = ActivationFunctionType
+
+SHORT, GATHER, HOP, LOAD, FAR = 0.06, 0.22, 0.22, 1.6, 2.0
+PICKS = ("vvss", "vvss")
+
+
+def in_order(calls):
+    before, wrote, readers = [], {}, {}
+    for i, c in enumerate(calls):
+        deps = {wrote[k] for k in c["rd"] + c["wr"] + c["after"] if k in wrote}
+        for k in c["wr"]:
+            deps.update(readers.get(k, []))
+        before.append(deps)
+        for k in c["rd"]:
+            readers.setdefault(k, []).append(i)
+        for k in c["wr"]:
+            wrote[k], readers[k] = i, []
+    ahead = [c["hold"] + c["lag"] for c in calls]
+    for i in reversed(range(len(calls))):
+        for d in before[i]:
+            ahead[d] = max(ahead[d], calls[d]["hold"] + calls[d]["lag"] + ahead[i])
+    for i, c in enumerate(calls):
+        if c["kind"] == "dma" and not before[i]:
+            ahead[i] = 1e3 - i
+    free, done, order, left = {}, {}, [], set(range(len(calls)))
+    while left:
+        can = {i: max([free.get(calls[i]["q"], 0.0)] + [done[d] for d in before[i]]) for i in left if all(d in done for d in before[i])}
+        soonest = min(can, key=lambda i: (can[i], i))
+        rivals = [i for i in can if calls[i]["q"] == calls[soonest]["q"] and can[i] <= can[soonest] + SLACK * calls[soonest]["hold"]]
+        i = max(rivals, key=lambda i: (ahead[i], -i))
+        free[calls[i]["q"]] = can[i] + calls[i]["hold"]
+        done[i] = can[i] + calls[i]["hold"] + calls[i]["lag"]
+        order.append(calls[i])
+        left.remove(i)
+    return order
+
+
+SLACK = 0.5
 
 
 def rank_program(g, core, T, topo):
@@ -53,13 +94,253 @@ def rank_program(g, core, T, topo):
         return
     cores = T.cores
     n = len(cores)
+    V, S, P = g.vector, g.scalar, g.tensor
+    Q = {"v": V, "s": S, "p": P, "g": g, "y": g.sync}
+    calls = []
 
-    Q = {"v": g.vector, "s": g.scalar, "p": g.tensor, "g": g, "y": g.sync}
-    csem = {"v": "cv", "s": "cs", "p": "cp", "g": "cg"}
-    count = {}
+    def call(q, fn, args, rd, wr, hold=SHORT, lag=HOP, kind="compute", after=(), **kw):
+        calls.append(dict(q=q, fn=fn, args=args, kw=kw, rd=list(rd), wr=list(wr), hold=hold, lag=lag, kind=kind, after=list(after)))
+
+    def dma(q, out, in_, rd, wr, lag=LOAD):
+        call(q, Q[q].dma_start, (out, in_), rd, wr, lag=lag, kind="dma")
+
+    def act(out, in_, func, rd, wr, hold, **kw):
+        call("s", S.activation, (out, in_, func), rd, wr, hold, **kw)
+
+    def copy(q, out, in_, rd, wr, hold=SHORT):
+        if q == "v":
+            call("v", V.tensor_copy, (out, in_), rd, wr, hold)
+        else:
+            act(out, in_, F.Copy, rd, wr, hold)
+
+    def ts(out, in0, s1, s2, op0, op1, rd, wr, hold=SHORT):
+        call("v", V.tensor_scalar, (out, in0, s1, s2, op0) + ((op1,) if op1 is not None else ()), rd, wr, hold)
+
+    def tt(out, in0, in1, op, rd, wr, hold=SHORT):
+        call("v", V.tensor_tensor, (out, in0, in1, op), rd, wr, hold)
+
+    def turn(out, in_, rd, wr, hold=SHORT):
+        call("v", V.transpose, (out, in_), rd, wr, hold)
+
+    def scan(out, d0, d1, rd, wr):
+        call("v", V.tensor_tensor_scan, (out, d0, d1, 0.0, A.mult, A.add), rd, wr)
+
+    def quant(q, s, x, rd, wr):
+        call("v", V.quantize_mx, (q, s, x), rd, wr, 0.14)
+
+    def product(b, stat, stat_s, mov, mov_s, rd):
+        call("p", P.matmul_mx, (bank(b), stat, stat_s, mov, mov_s, True, True), rd, [("ps", b)], 0.15)
+
+    def fill(ap, val, rd, key, hold=SHORT):
+        call("v", V.memset, (ap, val), rd, [key], hold)
+
+    def iota(out, pattern, base, key, hold=0.17):
+        call("g", g.iota, (out, pattern, base, 0), [], [key], hold, allow_small_or_imprecise_dtypes=True)
+
+    def u8(ap):
+        return ap.bitcast(dt.uint8)
+
+    def u32(ap):
+        return ap.bitcast(dt.uint32)
+
+    def bank(b):
+        return T.ps[:, 512 * b:512 * b + H]
+
+    def engines_of(r):
+        m = -1
+        for t in range(R):
+            m &= topo.mask(cores[r], cores[(r + 1 + t) % n])
+        return m
+
+    def ones(m):
+        return bin(m).count("1")
+
+    def half(buf, h, a=0, step=1, p0=0, p1=128, w=H, end=None):
+        return buf[p0:p1, w * h + a:w * h + (w if end is None else end):step]
+
+    def lst(buf, h, a=0, step=1, p0=0, p1=128, end=None):
+        return half(buf, h, a, step, p0, p1, 8, end)
+
+    X = [T["xs%d" % t] for t in range(R + 1)]
+    xk = lambda t, h: [("x", t, h, b) for b in range(4)]
+
+    dma("s", T.raw[:], T.ct[:], [], ["raw"], 1.1)
+    dma("y", T.ut[:], T.u[:], [], ["ut"])
+    dma("s", X[0][:, 0:512], T.x[:, 0:512], [], xk(0, 0), 2.0)
+    dma("y", X[0][:, 512:1024], T.x[:, 512:1024], [], xk(0, 1), 2.4)
+    for h in range(2):
+        dma("y", X[0][:, 1024 + 512 * h:1536 + 512 * h], T.x[:, 512 * h:512 * h + 512], [], [("xd", 0, h)], 3.5)
+    dma("y", u8(T.wq[:]), T.wc[:], [], ["wq"])
+    dma("y", T.wp[:], T.ws[:], [], ["wp"])
+    dma("y", T.vt[:], T.v[:], [], ["vt"], 6.0)
+
+    ucol, eps, p15, k16, is15, is1, dcon = range(0, 224, 32)
+    at = lambda c, p0=0, p1=128: T.kt[p0:p1, c:c + 1]
+    row16 = lambda p0=0, p1=128: T.kk[p0:p1, p15:p15 + 16]
+    iota(T.kk[:, ucol:ucol + 32], [[0, 2], [16, 4], [1, 4]], 0, "k0")
+    iota(T.row[:, 0:4], [[32, 4]], 0, "r0")
+    iota(T.row[:, 4:8], [[0, 2], [64, 2]], 0, "r1")
+    iota(T.kk[:, p15:p15 + 32], [[0, 2], [1, 16]], 0, "k1")
+    iota(T.col[:], [[1, 256]], 0, "col", 0.6)
+    iota(T.row[:, 16:32], [[64, 4], [16, 2], [0, 2]], 0, "r2")
+    iota(T.wj[:], [[1, 288]], -255, "wj", 0.7)
+    iota(T.wb[:, 256:512], [[1, 16], [16, 16]], 0, "wb1", 0.6)
+    fill(T.kk[:, eps:eps + 32], 0.0, [], "kz0")
+    fill(T.kk[:, k16:224], 0.0, [], "kz1", 0.12)
+    first = [(eps + 8, eps + 12, 80.0), (eps + 24, eps + 28, 80.0), (eps + 12, eps + 16, -48.0), (eps + 28, eps + 32, -48.0)]
+    for i, (a, b, val) in enumerate(first):
+        fill(T.kk[:, a:b], val, ["kz0"], ("ke", i))
+    turn(T.kt[:, 0:64], T.kk[:, 0:64], ["k0", "kz0"] + [("ke", i) for i in range(4)], ["kt0"])
+    pieces = [(T.kk[:, k16 + 16:k16 + 32], 16.0), (T.kk[:, is15 + 15:is15 + 32:16], 1.0), (T.kk[:, is1 + 1:is1 + 32:16], 1.0),
+              (T.kk[64:128, dcon:dcon + 15], -16.0), (T.kk[64:128, dcon + 16:dcon + 31], -16.0), (T.kk[64:128, dcon + 15:dcon + 32:16], 240.0)]
+    for i, (ap, val) in enumerate(pieces):
+        fill(ap, val, ["kz1"], ("kp", i))
+    turn(T.kt[:, 64:224], T.kk[:, 64:224], ["k1", "kz1"] + [("kp", i) for i in range(len(pieces))], ["kt"], 0.15)
+    fill(T.dd[:], 2.0, [], "dd")
+    fill(T.dd[:, 0:128:8], 0.0, ["dd"], "dd0")
+    fill(T.dd[:, 4:128:8], 1.0 / 128, ["dd"], "dd4")
+    fill(T.lt[:], 0, [], "ltz")
+    fill(T.one[0:96, 0:8], 1.0, [], "one0")
+    fill(T.one[96:128, 0:8], 16.0, [], "one1")
+    fill(T.one[:, 8:16], -TINY, [], "one2")
+    fill(T.ty[:, 32:48], 0.0, [], "tyz")
+    fill(T.tin[:], 0.0, [], "tinz")
+    ts(T.ucl[:, 0:1], at(ucol), at(eps), None, A.add, None, ["kt0"], ["uc0"])
+    ts(T.ucl[:, 1:8], T.row[:, 1:8], at(ucol), 127.0, A.add, A.min, ["kt0", "r0", "r1"], ["uc1"])
+    ts(T.km[64:128, :], row16(64), at(p15, 64), None, A.is_lt, None, ["kt"], ["km1"])
+    ts(T.km[0:64, :], row16(0, 64), at(k16, 0, 64), at(is1, 0, 64), A.add, A.mult, ["kt"], ["km0"])
+    for i in range(2):
+        ts(T.lt[0:64, 32 * i:32 * i + 16], row16(0, 64), 16.0, at(p15, 0, 64), A.mult, A.add, ["kt", "ltz"], [("ltj", i)])
+        act(T["k%d" % i][:], T.col[:], F.Identity, ["kt", "col"], [("kd", i)], 0.25, scale=at(is15), bias=at(dcon))
+    ts(T.one[:, 16:17], at(k16), 2.0, at(p15), A.mult, A.add, ["kt"], ["pj"])
+    ts(T.l7[:], T.row[:, 16:32], T.one[:, 16:17], None, A.add, None, ["pj", "r2"], [("l7", h, i) for h in range(2) for i in range(2)])
+
+    for i in range(2):
+        copy("v", T.tn[:, 16 * i:16 * i + 16], T.raw[:], ["raw"], [("tn", i)])
+    turn(T.ty[:, 0:32], T.tn[:], [("tn", 0), ("tn", 1)], ["ty"])
+    moves = [(64, 0, 0, 0, 32), (96, 0, 0, 0, 32), (0, 16, 96, 16, 16), (64, 32, 32, 0, 32), (96, 32, 32, 0, 32), (96, 64, 96, 0, 16)]
+    for i, (p0, c0, p1, c1, w) in enumerate(moves):
+        copy("v", T.lt[p0:p0 + 32, c0:c0 + w], T.ty[p1:p1 + 32, c1:c1 + w], ["ty", "ltz"], [("lt", i)])
+    for i, (c0, c1, w) in enumerate([(0, 0, 15), (16, 0, 15), (32, 16, 16), (48, 16, 16)]):
+        tt(T.tz[96:128, c0:c0 + w], T.ty[64:96, c1:c1 + w], T.ty[64:96, c1 + 1:c1 + 1 + w], A.subtract, ["ty", "tyz"], [("tz", i)])
+    ts(T.tz[96:128, 15:32:16], T.ty[64:96, 0:2], 0.0, T.ty[64:96, 15:16], A.mult, A.add, ["ty"], [("tz", 4)])
+    for i in range(2):
+        turn(T["k%d" % i][96:128, 0:32], T.tz[96:128, 32 * i:32 * i + 32], [("tz", k) for k in ((0, 1, 4), (2, 3))[i]], [("kd", i)])
+        act(T.wm[:, 256 * i:256 * i + 256], T.km[:].indirect(T.lt[:, 32 * i + 16:32 * i + 32]), F.Copy,
+            [("lt", k) for k in ((0, 1, 2), (3, 4))[i]] + ["km0", "km1"], [("wm", i)], 2 * GATHER)
+    act(T.wd[:, 0:256], T.k0[:].indirect(T.lt[:, 0:16]), F.Copy, [("lt", 0), ("lt", 1), ("ltj", 0), ("kd", 0)], [("wd", 0)], 2 * GATHER)
+    act(T.wd[:, 256:512], T.k1[:].indirect(T.lt[:, 32:48]), F.Copy, [("lt", 3), ("lt", 4), ("ltj", 1), ("kd", 1), "one0", "one1"], [("wd", 1)],
+        2 * GATHER, scale=T.one[:, 0:1])
+    act(T.wb[:, 0:256], T.col[:].indirect(T.lt[:, 64:80]), F.Copy, [("lt", 5), "col"], ["wb0"], 2 * GATHER, scale=16.0)
+
+    quant(T.qu[:], T.su[:], T.ut[:], ["ut"], ["qu"])
+    copy("v", u32(T.qup[:]), u32(T.qu[:]).indirect(T.ucl[:]), ["qu", "uc0", "uc1"], ["qup"], GATHER)
+    copy("s", T.sup[:], T.su[:].indirect(T.ucl[:]), ["qu", "uc0", "uc1"], ["sup"], GATHER)
+    quant(T.qv[:], T.sv[:], T.vt[:], ["vt"], ["qv"])
+
+    def state(t, h):
+        if t:
+            for b in range(4):
+                tt(half(X[t], h, b, 4, w=512), T.hh[:, 256 * b:256 * b + 256].indirect(lst(T.lsib, h)), half(X[t - 1], h, b, 4, w=512), A.add,
+                   [("h", b, 0), ("h", b, 1), "lsib", ("x", t - 1, h, b)], [("x", t, h, b)], GATHER)
+        if 0 < t < R:
+            call("g", g.affine_select, (half(X[t], h + 2, w=512), half(X[t], h, w=512), [[0, 512]], A.is_ge, 0.0, 0, 0),
+                 xk(t, h), [("xd", t, h)], 1.2)
+        qx, sx = half(T["qx%d" % t], h), half(T["sx%d" % t], h)
+        quant(qx, sx, half(X[t], h, w=512), xk(t, h), [("qx", t, h)])
+        stat, scale, keys = (T.qup, T.sup, ["qup", "sup"]) if t < R else (T.qv, T.sv, ["qv"])
+        product(h, stat[:], scale[:], qx, sx, keys + [("qx", t, h)])
+
+    def places(t, h):
+        act(half(T.bits, h), bank(h), F.Sign, ["one2"], [("ps", h), ("bits", h)], 0.13, bias=T.one[:, 8:9])
+        turn(half(T.bt, h), half(T.bits, h), [("bits", h)], [("bt", h)])
+        scan(half(T.sc, h), T.dd[:], half(T.bt, h), [("bt", h), "dd0", "dd4"], [("sc", h)])
+        for k, pos, q in (("d", 7, "s"), ("m", 15, "v")):
+            for i in range(2):
+                ts(lst(T["l" + k], h, 4 * i, end=4 * i + 4), half(T.sc, h, pos + 16 * i, 32), 8.0, 127.5 + 256 * i, A.mult, A.add,
+                   [("sc", h)], [("l" + k, h, i)])
+            copy(q, half(T["f" + k], h), T["w" + k][:].indirect(lst(T["l" + k], h)),
+                 [("l" + k, h, 0), ("l" + k, h, 1), ("w" + k, 0), ("w" + k, 1)], [("f" + k, h)], GATHER)
+            turn(half(T["t" + k], h), half(T["f" + k], h), [("f" + k, h)], [("t" + k, h)])
+        scan(half(T.s2, h), half(T.tm, h), half(T.td, h), [("tm", h), ("td", h)], [("s2", h), ("a6", h)])
+        for i in range(2):
+            ts(lst(T.l7, h, 4 * i + 1, 2, 96, end=4 * i + 4), half(T.tm, h, 32 * i + 1, 16, 0, 32, end=32 * i + 32), T.one[0:32, 16:17],
+               128.0 * h + 64 * i, A.add, A.add, [("tm", h), "pj"], [("l7", h, i)])
+        copy("s", half(T.f7, h), T.wj[:].indirect(lst(T.l7, h)), [("l7", h, 0), ("l7", h, 1), "wj"], [("f7", h)], GATHER)
+        six = half(T.s2, h, 15, 16, 96, end=64)
+        tt(six, six, half(T.s2, h, 79, 16, 96), A.add, [("s2", h)], [("a6", h)])
+        ts(lst(T.l3, h, 1, 2, 0, 96), half(T.s2, h, 79, 16, 0, 96), 256.0, None, A.add, None, [("s2", h)], [("l3", h, 2)])
+        for i in range(2):
+            ts(lst(T.l3, h, i, 2, 96 * i), half(T.s2, h, 15, 16, 96 * i, end=64), 256.0 * (1 - i), None, A.add, None,
+               [("s2", h), ("a6", h)], [("l3", h, i)])
+        tt(half(T.f3, h), T.wb[:].indirect(lst(T.l3, h)), half(T.f7, h), A.add,
+           [("l3", h, k) for k in range(3)] + [("f7", h), "wb0", "wb1"], [("f3", h)], GATHER)
+        turn(half(T.t3, h), half(T.f3, h), [("f3", h)], [("t3", h)])
+
+    mymask = engines_of(rank)
+
+    def send(t, h):
+        for e in (2, 3, 0, 1):
+            ts(lst(T.lz, 2 * e + h), half(T.t3, h, 0, 16), 4.0, 1020.0 + e, A.mult, A.add, [("t3", h)], [("lz", e, h)])
+            copy(PICKS[h][e], half(T["zz%d" % t], h, e, 4, w=512), X[t][:, 0:1536 + 512 * h].indirect(lst(T.lz, 2 * e + h)),
+                 xk(t, 0) + xk(t, 1) + [("xd", t, k) for k in range(h + 1)] + [("lz", e, h)], [("z", t, e, h)], GATHER)
+        qz, sz = half(T["qz%d" % t], h), half(T["sz%d" % t], h)
+        quant(qz, sz, half(T["zz%d" % t], h, w=512), [("z", t, e, h) for e in range(4)], [("qz", t, h)])
+        rid, pid, _ = topo.addr(cores[(rank + 1 + t) % n])
+        for i, (dst, src) in enumerate(((u8(half(T["lq%d" % t], h)), u8(qz)), (half(T["ls%d" % t], h), sz))):
+            call("g", g.remote_dma, (dst, src, T.sem["arr%d%d" % (t, h)], T.sem.sent, pid, rid, mymask), [("qz", t, h)], [("far", t, h, i)],
+                 0.2, FAR + (1 - h), "remote")
+
+    def layer(t, h):
+        call("p", None, ("arr%d%d" % (t, h), NCALL * ones(engines_of((rank - 1 - t) % n))), [], [("lq", t, h)], 0.0, 0.0, "arrive",
+             after=[("far", t, h, i) for i in range(NCALL)])
+        for b in range(4):
+            k = 4 * h + b
+            product(k, half(T.wq, b), half(T.wp, b), half(T["lq%d" % t], h), half(T["ls%d" % t], h), ["wq", "wp", ("lq", t, h)])
+            if h == 1 and b == 0:
+                ts(half(T.hh, 2 * b + h), bank(k), 0.03125, None, A.mult, None, [], [("ps", k), ("h", b, h)], 0.13)
+            else:
+                act(half(T.hh, 2 * b + h), bank(k), F.Copy, [], [("ps", k), ("h", b, h)], 0.13, scale=0.03125)
+
+    def sibling(t):
+        for i, k in enumerate((0, 2, 1, 3)):
+            ts(T.wi[:, i:16:4], T.t3[:, 16 * k:256:64], 255.0, None, A.add, None, [("t3", 0), ("t3", 1)], [("wi", i)])
+        wik = [("wi", i) for i in range(4)]
+        ts(T.wa[:, 0:16], T.wi[:], 223, None, A.bitwise_and, None, wik, ["wa0"])
+        ts(T.wa[:, 16:32], T.wi[:], 16, None, A.bitwise_and, None, wik, ["wa1"])
+        ts(T.wa[:, 32:48], T.wi[:], 1, 16, A.logical_shift_right, A.bitwise_and, wik, ["wa2"])
+        tt(T.tin[:, 0:16], T.wa[:, 0:16], T.wa[:, 16:32], A.add, ["wa0", "wa1", "tinz"], ["tin0"])
+        copy("v", T.tin[:, 32:48], T.wa[:, 32:48], ["wa2", "tinz"], ["tin1"])
+        turn(T.y1[:], T.tin[:], ["tin0", "tin1"], ["y1"])
+        for i in range(2):
+            tt(T.y2[:, 16 * i:16 * i + 16], T.y1[:, 16 - 16 * i:32 - 16 * i], T.y1[:, 48 - 16 * i:64 - 16 * i], A.add, ["y1"], [("y2", i)])
+        turn(T.y3[:], T.y2[:], [("y2", 0), ("y2", 1)], ["y3"])
+        copy("v", T.lsib[:], T.y3[:, 0:16], ["y3"], ["lsib"])
+        if t == R - 1:
+            ts(T.wa[:, 48:64], T.wi[:], 255, None, A.bitwise_and, None, wik, ["wa3"])
+            copy("v", T.lown[:], T.wa[:, 48:64], ["wa3"], ["lown"])
+            copy("s", T.lof[:], T.col[:].indirect(T.lown[:]), ["lown", "col"], ["lof"], 2 * GATHER)
+            dma("y", T.lo[:], T.lof[0:128:16, :], ["lof"], ["lo"])
+
+    for t in range(R):
+        for step in (state, places, send):
+            for h in range(2):
+                step(t, h)
+        sibling(t)
+        for h in range(2):
+            layer(t, h)
+
+    qx, sx = T["qx%d" % R], T["sx%d" % R]
+    for h in range(2):
+        state(R, h)
+        dma("y", half(T.oc, h, w=512), u8(half(qx, h)), [("qx", R, h)], [("oc", h)])
+        copy("sv"[h], half(T.yo, h), bank(h), [], [("ps", h), ("yo", h)], 0.13)
+        dma("s", half(T.y, h), half(T.yo, h), [("yo", h)], [("y", h)])
+    for k in range(4):
+        dma("sy"[k % 2], T.osc[4 * k:4 * k + 4, :], sx[32 * k:32 * k + 4, :], [("qx", R, 0), ("qx", R, 1)], [("osc", k)])
+
+    count, wrote, readers = {}, {}, {}
     known = {q: {} for q in Q}
-    wrote, readers = {}, {}
-    ndma = [0]
 
     def wait(q, tok):
         sem, c, snap = tok
@@ -72,255 +353,29 @@ def rank_program(g, core, T, topo):
             if k.get(s2, 0) < c2:
                 k[s2] = c2
 
-    def run(q, fn, rd, wr, dma=False):
-        deps = []
-        for key in rd:
-            if key in wrote:
-                deps.append(wrote[key])
-        for key in wr:
-            if key in wrote:
-                deps.append(wrote[key])
-            deps.extend(readers.get(key, []))
-        deps.sort(key=lambda tk: -tk[1])
-        for tk in deps:
+    ndma = 0
+    for c in in_order(calls):
+        q = c["q"]
+        deps = [wrote[k] for k in c["rd"] + c["wr"] if k in wrote] + [tk for k in c["wr"] for tk in readers.get(k, [])]
+        for tk in sorted(deps, key=lambda tk: -tk[1]):
             wait(q, tk)
-        if dma:
-            sem, inc = "d%d" % ndma[0], 16
-            ndma[0] += 1
-        else:
-            sem, inc = csem[q], 1
-        fn().then_inc(T.sem[sem], inc)
+        if c["kind"] == "arrive":
+            count[c["args"][0]] = c["args"][1]
+            wait(q, c["args"] + ({},))
+            continue
+        made = c["fn"](*c["args"], **c["kw"])
+        if c["kind"] == "remote":
+            count["sent"] = count.get("sent", 0) + ones(mymask)
+            continue
+        sem, inc = ("d%d" % ndma, 16) if c["kind"] == "dma" else ("c" + q, 1)
+        ndma += c["kind"] == "dma"
+        made.then_inc(T.sem[sem], inc)
         count[sem] = count.get(sem, 0) + inc
         tok = (sem, count[sem], dict(known[q]))
-        for key in rd:
-            readers.setdefault(key, []).append(tok)
-        for key in wr:
-            wrote[key] = tok
-            readers[key] = []
-        return tok
-
-    V, S, P = g.vector, g.scalar, g.tensor
-
-    def v(fn, rd, wr):
-        return run("v", fn, rd, wr)
-
-    def s(fn, rd, wr):
-        return run("s", fn, rd, wr)
-
-    def dma(q, out, in_, rd, wr):
-        return run(q, lambda: Q[q].dma_start(out, in_), rd, wr, dma=True)
-
-    def u8(ap):
-        return ap.bitcast(dt.uint8)
-
-    def u32(ap):
-        return ap.bitcast(dt.uint32)
-
-    def bank(b, w):
-        return T.ps[:, 512 * b:512 * b + w]
-
-    def engines_of(r):
-        m = -1
-        for t in range(R):
-            m &= topo.mask(cores[r], cores[(r + 1 + t) % n])
-        return m
-
-    def ones(m):
-        return bin(m).count("1")
-
-    X = [T["xs%d" % t] for t in range(R + 1)]
-    xk = lambda t: [("x", t, b) for b in range(4)]
-    xdk = lambda t: [("xd", t, b) for b in range(4)]
-
-    dma("y", T.ut[:], T.u[:], [], ["ut"])
-    dma("s", X[0][:, 0:512], T.x[:, 0:512], [], ["x0h0"])
-    dma("y", X[0][:, 512:1024], T.x[:, 512:1024], [], ["x0h1"])
-    v(lambda: V.memset(T.raw[64:128, 0:256], 0), [], ["rawA"])
-    v(lambda: V.memset(T.raw[64:128, 256:512], 0), [], ["rawB"])
-    run("g", lambda: g.iota(T.kk[:, 128:160], [[0, 2], [1, 16]], 0, 0, allow_small_or_imprecise_dtypes=True), [], ["k4"])
-    for h in range(2):
-        run("g", lambda: g.iota(T.kk[:, 160 + 16 * h:176 + 16 * h], [[112, 2], [16, 2], [1, 4]], 0, 0,
-                                allow_small_or_imprecise_dtypes=True), [], [("k5", h)])
-    run("g", lambda: g.iota(T.raw[0:64, :], [[0, 2], [1, 16], [16, 16]], 0, 0), [], ["rawI"])
-    run("g", lambda: g.iota(T.wt[:, 512:768], [[1, 256]], 0, 0, allow_small_or_imprecise_dtypes=True), [], ["wtI"])
-    pieces = [("s", 64, 0, 0, 6), ("y", 80, 0, 0, 6), ("s", 96, 0, 0, 1), ("y", 112, 0, 0, 1),
-              ("s", 65, 1, 3, 1), ("y", 81, 1, 3, 1), ("s", 96, 1, 2, 6), ("y", 112, 1, 2, 6)]
-    rawk = [[], []]
-    for i, (q, p0, h, t0, nt) in enumerate(pieces):
-        dma(q, T.raw[p0:p0 + nt, 256 * h:256 * h + 256], T.ct[16 * t0:16 * (t0 + nt), :], ["rawA" if h == 0 else "rawB"], [("raw", i)])
-        rawk[h].append(("raw", i))
-    dma("y", X[0][:, 1024:2048], T.x[:], [], xdk(0))
-    dma("y", u8(T.wq[:]), T.wc[:], [], ["wq"])
-    dma("y", T.wp[:], T.ws[:], [], ["wp"])
-    dma("y", T.vt[:], T.v[:], [], ["vt"])
-
-    v(lambda: V.memset(T.kk[:, 0:96], 0.0), [], ["k0"])
-    v(lambda: V.memset(T.kk[:, 96:128], 1.0), [], ["k3"])
-    v(lambda: V.memset(T.kk[:, 8:16], 1e29), ["k0"], ["k0a"])
-    v(lambda: V.memset(T.kk[:, 32:48:8], -2.0), ["k0"], ["k0b"])
-    v(lambda: V.memset(T.kk[:, 64:72], 32.0), ["k0"], ["k0c"])
-    v(lambda: V.memset(T.kk[:, 80:88], 32.0), ["k0"], ["k0d"])
-    v(lambda: V.memset(T.kk[:, 96:128:4], 16.0), [], ["k3"])
-    v(lambda: V.memset(T.dd[:], 2.0), [], ["dd"])
-    v(lambda: V.transpose(T.kt[:], T.kk[:]), ["k0", "k0a", "k0b", "k0c", "k0d", "k3", "k4", ("k5", 0), ("k5", 1)], ["kt"])
-    v(lambda: V.memset(T.dd[:, 0:128:8], 0.0), [], ["dd"])
-    thr, add0, lo32, scl, p15, gu = [T.kt[:, 32 * i:32 * i + 1] for i in range(6)]
-    Rw = lambda a, b, c=1: T.kk[:, 128 + a:128 + b:c]
-    for i, (a, b, src) in enumerate([(0, 4, Rw(0, 4)), (4, 6, Rw(1, 4, 2)), (6, 8, Rw(0, 4, 2))]):
-        v(lambda: V.tensor_scalar(T.uci[:, a:b], src, lo32, gu, A.mult, A.add), ["kt"], [("uci", i)])
-    v(lambda: V.tensor_scalar(T.p16[:, 0:1], p15, 16.0, None, A.mult), ["kt"], ["p16"])
-    v(lambda: V.tensor_scalar(T.ucm[:], T.uci[:], 127, None, A.bitwise_and), [("uci", i) for i in range(3)], ["ucm"])
-    v(lambda: V.tensor_scalar(T.swl[:], Rw(0, 16), T.p16[:, 0:1], None, A.add), ["p16"], ["swl"])
-    v(lambda: V.tensor_copy(T.ucl[:], T.ucm[:]), ["ucm"], ["ucl"])
-
-    v(lambda: V.quantize_mx(T.qu[:], T.su[:], T.ut[:]), ["ut"], ["qu"])
-    v(lambda: V.tensor_scalar(T.jj[:], Rw(0, 16), 16.0, p15, A.mult, A.add), ["kt"], ["jj"])
-    v(lambda: V.tensor_copy(u32(T.qup[:]), u32(T.qu[:]).indirect(T.ucl[:, 0:8])), ["qu", "ucl"], ["qup"])
-    s(lambda: S.activation(T.sup[:], T.su[:].indirect(T.ucl[:, 0:8]), COPY), ["qu", "ucl"], ["sup"])
-
-    def table(h):
-        v(lambda: V.tensor_scalar(T.wt[:, 256 * h:256 * h + 256], T.raw[:, 256 * h:256 * h + 256].indirect(T.swl[:]), scl, None, A.mult),
-          rawk[h] + ["rawI", "swl", "kt"], [("wt", h)])
-
-    def quant_x(t):
-        for h in range(2):
-            v(lambda: V.quantize_mx(T["qx%d" % t][:, 128 * h:128 * h + 128], T["sx%d" % t][:, 128 * h:128 * h + 128],
-                                    X[t][:, 512 * h:512 * h + 512]),
-              ["x0h%d" % h] if t == 0 else xk(t), [("qx", t, h)])
-
-    def product(stat, scale, keys, t):
-        for h in range(2):
-            run("p", lambda: P.matmul_mx(bank(5 + h, 128), stat, scale, T["qx%d" % t][:, 128 * h:128 * h + 128],
-                                         T["sx%d" % t][:, 128 * h:128 * h + 128], True, True),
-                keys + [("qx", t, h)], [("ps", 5 + h)])
-
-    def lookup(lst, lk, win, wk, f, fk, tt, tk, between):
-        v(lambda: V.tensor_copy(f[:, 0:128], win.indirect(lst[:, 0:8])), lk + wk, [(fk, 0)])
-        s(lambda: S.activation(f[:, 128:256], win.indirect(lst[:, 8:16]), COPY), lk + wk, [(fk, 1)])
-        between()
-        v(lambda: V.transpose(tt[:], f[:]), [(fk, 0), (fk, 1)], [tk])
-
-    mymask = engines_of(rank)
-    sent = 0
-    win12, win3, winI = T.wt[:, 0:512], T.wt[:, 256:768], T.wt[:, 512:768]
-    w12, w3 = [("wt", 0), ("wt", 1)], [("wt", 1), "wtI"]
-
-    for t in range(R):
-        quant_x(t)
-        product(T.qup[:], T.sup[:], ["qup", "sup"], t)
-        if t == 0:
-            table(0)
-        for h in range(2):
-            v(lambda: V.tensor_scalar(T.bits[:, 128 * h:128 * h + 128], bank(5 + h, 128), thr, add0, A.is_gt, A.add),
-              ["kt"], [("ps", 5 + h), ("bits", h)])
-        for h in range(2):
-            v(lambda: V.transpose(T.bt[:, 128 * h:128 * h + 128], T.bits[:, 128 * h:128 * h + 128]), [("bits", h)], [("bt", h)])
-        for h in range(2):
-            v(lambda: V.tensor_tensor_scan(T.sc[:, 128 * h:128 * h + 128], T.dd[:], T.bt[:, 128 * h:128 * h + 128], 0.0, A.mult, A.add),
-              [("bt", h), "dd"], [("sc", h)])
-        if t == 0:
-            table(1)
-        sck = [("sc", 0), ("sc", 1)]
-        v(lambda: V.tensor_scalar(T.l1[:], T.sc[:, 7:256:16], 256.0, None, A.add), sck, ["l1", "l3a", "l3b"])
-
-        def b1():
-            v(lambda: V.tensor_scalar(T.l2[:], T.sc[:, 15:256:16], 256.0, None, A.add), sck, ["l2"])
-        lookup(T.l1, ["l1", "l3a", "l3b"], win12, w12, T.f1, "f1", T.t1, "t1", b1)
-        v(lambda: V.tensor_tensor(T.t1[64:96, 1:256:16], T.t1[64:96, 1:256:16], T.t1[96:128, 0:256:16], A.add), [], ["t1"])
-        v(lambda: V.tensor_copy(T.l2[64:96, :], T.t1[64:96, 1:256:16]), ["t1"], ["l2"])
-
-        def b2():
-            v(lambda: V.tensor_tensor(T.a1[0:96, :], T.t1[0:96, 1:256:16], T.jj[0:96, :], A.add), ["t1", "jj"], ["a1a"])
-        lookup(T.l2, ["l2"], win12, w12, T.f2, "f2", T.t2, "t2", b2)
-        v(lambda: V.tensor_tensor(T.a6[96:128, :], T.t2[64:96, 4:256:32], T.t2[64:96, 21:256:32], A.add), ["t2"], ["a6"])
-        v(lambda: V.tensor_tensor(T.ee[96:128, :], T.t2[96:128, 5:256:16], T.jj[96:128, :], A.add), ["t2", "jj"], ["ee"])
-        v(lambda: V.tensor_scalar(T.l1[96:128, 0:16:2], T.a6[96:128, :], 256.0, None, A.add), ["a6"], ["l3a"])
-        v(lambda: V.tensor_copy(T.l1[96:128, 1:16:2], T.a6[96:128, :]), ["a6"], ["l3b"])
-        lookup(T.l1, ["l1", "l3a", "l3b"], win3, w3, T.f3, "f3", T.t3, "t3", lambda: None)
-        v(lambda: V.tensor_tensor(T.a1[96:128, :], T.t3[96:128, 4:256:16], T.ee[96:128, :], A.add), ["t3", "ee"], ["a1c"])
-        a1k = ["a1a", "a1c"]
-
-        Z, qz, sz = T["zz%d" % t], T["qz%d" % t], T["sz%d" % t]
-        lq, ls = T["lq%d" % t], T["ls%d" % t]
-        xw = (["x0h0", "x0h1"] if t == 0 else xk(t)) + xdk(t)
-        rid, pid, _ = topo.addr(cores[(rank + 1 + t) % n])
-
-        def zpick(q, e, h):
-            out = Z[:, 512 * h + e:512 * h + 512:4]
-            src = X[t][:].indirect(T.lz[:, 16 * e + 8 * h:16 * e + 8 * h + 8])
-            fn = (lambda: V.tensor_copy(out, src)) if q == "v" else (lambda: S.activation(out, src, COPY))
-            run(q, fn, xw + [("lz", e)], [("z", t, e, h)])
-
-        def zquant(h):
-            return v(lambda: V.quantize_mx(qz[:, 128 * h:128 * h + 128], sz[:, 128 * h:128 * h + 128], Z[:, 512 * h:512 * h + 512]),
-                     [("z", t, e, h) for e in range(4)], [("qz", t, h)])
-
-        def send(dst, src):
-            g.remote_dma(dst, src, T.sem["arr%d" % t], T.sem.sent, pid, rid, mymask)
-
-        for e in (2, 3, 0, 1):
-            v(lambda: V.tensor_scalar(T.lz[:, 16 * e:16 * e + 16], T.a1[:], 4.0, float(e), A.mult, A.add), a1k, [("lz", e)])
-        for e, h in ((2, 0), (3, 0), (2, 1), (3, 1), (1, 1)):
-            zpick("s", e, h)
-        zpick("v", 0, 0)
-        zpick("v", 1, 0)
-        v(lambda: V.tensor_scalar(T.tin[:, 16:32], T.a1[:], 256.0, -256.0, A.is_ge, A.mult), a1k, ["ge"])
-        wait("g", zquant(0))
-        send(u8(lq[:, 0:128]), u8(qz[:, 0:128]))
-        zpick("v", 0, 1)
-        wait("g", zquant(1))
-        send(u8(lq[:, 128:256]), u8(qz[:, 128:256]))
-        send(ls[:], sz[:])
-        sent += NCALL * ones(mymask)
-
-        v(lambda: V.tensor_tensor(T.tin[:, 0:16], T.a1[:], T.tin[:, 16:32], A.add), a1k + ["ge"], ["tin"])
-        v(lambda: V.transpose(T.y1[:], T.tin[:]), ["tin", "ge"], ["y1"])
-        v(lambda: V.tensor_copy(T.y2[:, 0:16], T.y1[:, 16:32]), ["y1"], ["y2a"])
-        v(lambda: V.tensor_copy(T.y2[:, 16:32], T.y1[:, 0:16]), ["y1"], ["y2b"])
-        v(lambda: V.transpose(T.y3[:], T.y2[:]), ["y2a", "y2b"], ["y3"])
-        v(lambda: V.tensor_copy(T.lsib[:], T.y3[:, 0:16]), ["y3"], ["lsib"])
-        if t == 0:
-            v(lambda: V.quantize_mx(T.qv[:], T.sv[:], T.vt[:]), ["vt"], ["qv"])
-        if t == R - 1:
-            v(lambda: V.tensor_copy(T.lown[:], T.tin[:, 0:16]), ["tin"], ["lown"])
-            s(lambda: S.activation(T.lof[:], winI.indirect(T.lown[:]), COPY), ["lown", "wtI"], ["lof"])
-            dma("y", T.lo[:], T.lof[0:128:16, :], ["lof"], ["lo"])
-
-        got = NCALL * ones(engines_of((rank - 1 - t) % n))
-        count["arr%d" % t] = got
-        wait("p", ("arr%d" % t, got, {}))
-        jobs = [(0, 0, 0, 128), (1, 0, 128, 128), (2, 1, 0, 256), (3, 2, 0, 256), (4, 3, 0, 256)]
-        for bk, b, c0, w in jobs:
-            run("p", lambda: P.matmul_mx(bank(bk, w), T.wq[:, 128 * b:128 * b + 128], T.wp[:, 128 * b:128 * b + 128],
-                                         lq[:, c0:c0 + w], ls[:, c0:c0 + w], True, True), ["wq", "wp"], [("ps", bk)])
-        for bk, b, c0, w in jobs:
-            out = T.hh[:, 256 * b + c0:256 * b + c0 + w]
-            if bk == 0:
-                v(lambda: V.tensor_scalar(out, bank(bk, w), 0.03125, None, A.mult), [], [("ps", bk), ("h", bk)])
-            else:
-                s(lambda: S.activation(out, bank(bk, w), COPY, scale=0.03125), [], [("ps", bk), ("h", bk)])
-        for b in range(4):
-            hk = [("h", 0), ("h", 1)] if b == 0 else [("h", b + 1)]
-            v(lambda: V.tensor_tensor(X[t + 1][:, b:1024:4], T.hh[:, 256 * b:256 * b + 256].indirect(T.lsib[:]), X[t][:, b:1024:4], A.add),
-              hk + ["lsib"] + (["x0h0", "x0h1"] if t == 0 else [("x", t, b)]), [("x", t + 1, b)])
-            if t + 1 < R:
-                s(lambda: S.activation(X[t + 1][:, 1024 + b:2048:4], X[t + 1][:, b:1024:4], COPY), [("x", t + 1, b)], [("xd", t + 1, b)])
-
-    quant_x(R)
-    product(T.qv[:], T.sv[:], ["qv"], R)
-    qk = [("qx", R, 0), ("qx", R, 1)]
-    qx, sx = T["qx%d" % R], T["sx%d" % R]
-    dma("y", T.oc[:], u8(qx[:]), qk, ["oc"])
-    v(lambda: V.tensor_copy(T.yo[:, 0:128], bank(5, 128)), [], [("ps", 5), "yo0"])
-    v(lambda: V.tensor_copy(T.yo[:, 128:256], bank(6, 128)), [], [("ps", 6), "yo1"])
-    dma("s", T.osc[4:8, :], sx[32:36, :], qk, [("osc", 1)])
-    dma("s", T.osc[12:16, :], sx[96:100, :], qk, [("osc", 3)])
-    dma("y", T.osc[0:4, :], sx[0:4, :], qk, [("osc", 0)])
-    dma("s", T.y[:, 0:128], T.yo[:, 0:128], ["yo0"], ["y0"])
-    dma("y", T.y[:, 128:256], T.yo[:, 128:256], ["yo1"], ["y1o"])
-    dma("s", T.osc[8:12, :], sx[64:68, :], qk, [("osc", 2)])
-
-    count["sent"] = sent
+        for k in c["rd"]:
+            readers.setdefault(k, []).append(tok)
+        for k in c["wr"]:
+            wrote[k], readers[k] = tok, []
     for sem in sorted(count, key=lambda k: (k[0] == "d", len(k), k)):
         if not any(known[q].get(sem, 0) >= count[sem] for q in Q):
             wait("g", (sem, count[sem], {}))

@@ -12,37 +12,38 @@ SCRATCH = {
     "qv": ("sbuf", [128, 128], X4), "sv": ("sbuf", [128, 128], "uint8"),
     "wq": ("sbuf", [128, 512], X4), "wp": ("sbuf", [128, 512], "uint8"),
     "ps": ("psum", [128, 4096], "float32"),
-    "kk": ("sbuf", [128, 224], "float32"), "kt": ("sbuf", [128, 224], "float32"), "row": ("sbuf", [128, 32], "float32"),
-    "col": ("sbuf", [128, 256], "bfloat16"), "one": ("sbuf", [128, 24], "float32"), "ucl": ("sbuf", [128, 8], "uint16"),
+    "kk": ("sbuf", [128, 144], "float32"), "kt": ("sbuf", [128, 128], "float32"), "row": ("sbuf", [128, 32], "float32"),
+    "col": ("sbuf", [128, 256], "bfloat16"), "one": ("sbuf", [128, 48], "float32"), "ucl": ("sbuf", [128, 8], "uint16"),
     "raw": ("sbuf", [128, 16], "int32"), "tn": ("sbuf", [128, 32], "bfloat16"), "ty": ("sbuf", [128, 48], "bfloat16"),
     "tz": ("sbuf", [128, 64], "bfloat16"), "lt": ("sbuf", [128, 80], "uint16"),
-    "k0": ("sbuf", [128, 256], "bfloat16"), "k1": ("sbuf", [128, 256], "bfloat16"), "km": ("sbuf", [128, 16], "bfloat16"),
+    "kd": ("sbuf", [128, 256], "bfloat16"), "km": ("sbuf", [128, 48], "bfloat16"),
     "wd": ("sbuf", [128, 512], "bfloat16"), "wm": ("sbuf", [128, 512], "bfloat16"), "wb": ("sbuf", [128, 512], "bfloat16"),
     "wj": ("sbuf", [128, 288], "bfloat16"), "dd": ("sbuf", [128, 128], "bfloat16"),
     "bits": ("sbuf", [128, 256], "bfloat16"), "bt": ("sbuf", [128, 256], "bfloat16"), "sc": ("sbuf", [128, 256], "bfloat16"),
     "ld": ("sbuf", [128, 16], "uint16"), "lm": ("sbuf", [128, 16], "uint16"), "l3": ("sbuf", [128, 16], "uint16"),
-    "l7": ("sbuf", [128, 16], "uint16"),
+    "l7": ("sbuf", [128, 16], "uint16"), "lz": ("sbuf", [128, 16], "uint16"),
     "fd": ("sbuf", [128, 256], "bfloat16"), "fm": ("sbuf", [128, 256], "bfloat16"), "f3": ("sbuf", [128, 256], "bfloat16"),
     "td": ("sbuf", [128, 256], "bfloat16"), "tm": ("sbuf", [128, 256], "bfloat16"), "t3": ("sbuf", [128, 256], "bfloat16"),
     "f7": ("sbuf", [128, 256], "bfloat16"), "s2": ("sbuf", [128, 256], "bfloat16"),
-    "lz": ("sbuf", [128, 64], "uint16"), "wi": ("sbuf", [128, 16], "int32"), "wa": ("sbuf", [128, 64], "int32"),
+    "wi": ("sbuf", [128, 16], "int32"), "wa": ("sbuf", [128, 64], "int32"),
     "tin": ("sbuf", [128, 64], "bfloat16"), "y1": ("sbuf", [128, 64], "bfloat16"),
     "y2": ("sbuf", [128, 32], "bfloat16"), "y3": ("sbuf", [128, 32], "bfloat16"),
     "lsib": ("sbuf", [128, 16], "uint16"), "lown": ("sbuf", [128, 16], "uint16"), "lof": ("sbuf", [128, 256], "float32"),
     "hh": ("sbuf", [128, 1024], "float32"), "yo": ("sbuf", [128, 256], "float32"),
 }
 for _t in range(R + 1):
-    SCRATCH["xs%d" % _t] = ("sbuf", [128, 2048 if _t < R else 1024], "bfloat16")
+    SCRATCH["xs%d" % _t] = ("sbuf", [128, 1024], "bfloat16")
     SCRATCH["qx%d" % _t] = ("sbuf", [128, C], X4)
     SCRATCH["sx%d" % _t] = ("sbuf", [128, C], "uint8")
 for _t in range(R):
+    SCRATCH["xp%d" % _t] = ("sbuf", [128, 2048], "bfloat16")
     SCRATCH["zz%d" % _t] = ("sbuf", [128, 1024], "bfloat16")
     SCRATCH["qz%d" % _t] = ("sbuf", [128, C], X4)
     SCRATCH["sz%d" % _t] = ("sbuf", [128, C], "uint8")
     SCRATCH["lq%d" % _t] = ("sbuf", [128, C], X4)
     SCRATCH["ls%d" % _t] = ("sbuf", [128, C], "uint8")
 
-NDMA = 30
+NDMA = 44
 NCALL = 2
 SEMAPHORES = (["cv", "cs", "cp", "cg", "sent"] + ["arr%d%d" % (_t, _h) for _t in range(R) for _h in range(2)]
               + ["d%d" % _i for _i in range(NDMA)])
@@ -50,42 +51,45 @@ SEMAPHORES = (["cv", "cs", "cp", "cg", "sent"] + ["arr%d%d" % (_t, _h) for _t in
 A = AluOpType
 F = ActivationFunctionType
 
-SHORT, GATHER, HOP, LOAD, FAR = 0.06, 0.22, 0.22, 1.6, 2.0
 PICKS = ("vvss", "vvss")
+WIDE = (0, 3)
+
+ORDER = {
+    (0, "v"): "kz dd ltz k16 ke0 ke1 ke2 ke3 kt not15 km1 uc0 uc1 tn0 tn1 ltj0 ltj1 km0 ty l7 qu lt0 lt1 lt2 qup qx0 lt3 lt4 tz0 tz1 tz2 tz3 tz4 "
+              "qx1 kd3 lt5 bt0 wd0 sc0 wd1 lm00 lm01 ld00 ld01 bt1 fm0 sc1 tm0 td0 ld10 ld11 lm10 s20 lm11 l700 l701 a60 fm1 l302 l300 l301 "
+              "tm1 td1 f30 l710 s21 l711 t30 a61 lz0 l312 l310 l311 z00 z10 f31 qz0 t31 lz1 wi0 wi1 z01 wi2 z11 wi3 qz1",
+    (0, "s"): "raw x00 b0 s01 tiny tyz dd0 is15 pj dd4 s1 b1 tinz0 tinz1 sup wm0 wm1 wm2 bits0 wm3 wd3 bits1 wd2 fd0 wb00 wb01 fd1 f70 f71 z20 z30 z21 z31",
+    (0, "g"): "k0 k1 r0 r1 r2 kd wb1 wj xp00 xp01 xp02 xp03 xp10 xp11 xp12 xp13 col",
+    (1, "v"): "x00 x01 x02 x03 x10 qx0 x11 x12 x13 qx1 bt0 sc0 ld00 ld01 lm00 lm01 bt1 fm0 sc1 td0 tm0 lm10 lm11 ld10 ld11 l700 s20 fm1 l701 "
+              "a60 l302 tm1 td1 l300 l301 l710 s21 l711 f30 a61 l312 t30 l310 l311 lz0 f31 z00 t31 z10 lz1 qz0 z01 z11 wi0 wi1 qz1 wi2 wi3",
+    (1, "s"): "bits0 bits1 fd0 fd1 f70 f71 z20 z30 z21 z31",
+    (3, "v"): "x00 x01 x02 x03 x13 qx0 qx1 yo0 yo1",
+    (3, "s"): "osc0 osc2 y0",
+    (3, "y"): "oc0 oc1 osc1 osc3 y1",
+}
 
 
 def in_order(calls):
     before, wrote, readers = [], {}, {}
     for i, c in enumerate(calls):
-        deps = {wrote[k] for k in c["rd"] + c["wr"] + c["after"] if k in wrote}
-        for k in c["wr"]:
-            deps.update(readers.get(k, []))
-        before.append(deps)
+        before.append({wrote[k] for k in c["rd"] + c["wr"] if k in wrote} | {r for k in c["wr"] for r in readers.get(k, [])})
         for k in c["rd"]:
             readers.setdefault(k, []).append(i)
         for k in c["wr"]:
             wrote[k], readers[k] = i, []
-    ahead = [c["hold"] + c["lag"] for c in calls]
-    for i in reversed(range(len(calls))):
-        for d in before[i]:
-            ahead[d] = max(ahead[d], calls[d]["hold"] + calls[d]["lag"] + ahead[i])
-    for i, c in enumerate(calls):
-        if c["kind"] == "dma" and not before[i]:
-            ahead[i] = 1e3 - i
-    free, done, order, left = {}, {}, [], set(range(len(calls)))
-    while left:
-        can = {i: max([free.get(calls[i]["q"], 0.0)] + [done[d] for d in before[i]]) for i in left if all(d in done for d in before[i])}
-        soonest = min(can, key=lambda i: (can[i], i))
-        rivals = [i for i in can if calls[i]["q"] == calls[soonest]["q"] and can[i] <= can[soonest] + SLACK * calls[soonest]["hold"]]
-        i = max(rivals, key=lambda i: (ahead[i], -i))
-        free[calls[i]["q"]] = can[i] + calls[i]["hold"]
-        done[i] = can[i] + calls[i]["hold"] + calls[i]["lag"]
-        order.append(calls[i])
-        left.remove(i)
-    return order
 
-
-SLACK = 0.5
+    def place(i):
+        c = calls[i]
+        names = ORDER.get((c["phase"] if c["phase"] in (0, R) else 1, c["q"]), "").split()
+        return c["phase"], names.index(c["name"]) if c["name"] in names else len(names), i
+    queues = {q: sorted((i for i, c in enumerate(calls) if c["q"] == q), key=place) for q in "ysgvp"}
+    row, out = [], set()
+    while len(row) < len(calls):
+        i = next(v[0] for v in queues.values() if v and before[v[0]] <= out)
+        queues[calls[i]["q"]].pop(0)
+        row.append(calls[i])
+        out.add(i)
+    return row
 
 
 def rank_program(g, core, T, topo):
@@ -96,46 +100,49 @@ def rank_program(g, core, T, topo):
     n = len(cores)
     V, S, P = g.vector, g.scalar, g.tensor
     Q = {"v": V, "s": S, "p": P, "g": g, "y": g.sync}
-    calls = []
+    calls, phase = [], [0]
 
-    def call(q, fn, args, rd, wr, hold=SHORT, lag=HOP, kind="compute", after=(), **kw):
-        calls.append(dict(q=q, fn=fn, args=args, kw=kw, rd=list(rd), wr=list(wr), hold=hold, lag=lag, kind=kind, after=list(after)))
+    def call(q, fn, args, rd, wr, kind="compute", name=None, **kw):
+        key = ([k for k in wr if k[0] != "ps"] + wr)[0]
+        if not isinstance(key, str):
+            key = key[0] + "".join(str(k) for k in key[1 + (key[0] in ("x", "xp", "xd", "qx", "z", "qz", "far", "lq")):])
+        calls.append(dict(name=name or key, phase=phase[0], q=q, fn=fn, args=args, kw=kw, rd=list(rd), wr=list(wr), kind=kind))
 
-    def dma(q, out, in_, rd, wr, lag=LOAD):
-        call(q, Q[q].dma_start, (out, in_), rd, wr, lag=lag, kind="dma")
+    def dma(q, out, in_, rd, wr):
+        call(q, Q[q].dma_start, (out, in_), rd, wr, "dma")
 
-    def act(out, in_, func, rd, wr, hold, **kw):
-        call("s", S.activation, (out, in_, func), rd, wr, hold, **kw)
+    def act(out, in_, func, rd, wr, **kw):
+        call("s", S.activation, (out, in_, func), rd, wr, **kw)
 
-    def copy(q, out, in_, rd, wr, hold=SHORT):
+    def copy(q, out, in_, rd, wr):
         if q == "v":
-            call("v", V.tensor_copy, (out, in_), rd, wr, hold)
+            call("v", V.tensor_copy, (out, in_), rd, wr)
         else:
-            act(out, in_, F.Copy, rd, wr, hold)
+            act(out, in_, F.Copy, rd, wr)
 
-    def ts(out, in0, s1, s2, op0, op1, rd, wr, hold=SHORT):
-        call("v", V.tensor_scalar, (out, in0, s1, s2, op0) + ((op1,) if op1 is not None else ()), rd, wr, hold)
+    def ts(out, in0, s1, s2, op0, op1, rd, wr, **kw):
+        call("v", V.tensor_scalar, (out, in0, s1, s2, op0) + ((op1,) if op1 is not None else ()), rd, wr, **kw)
 
-    def tt(out, in0, in1, op, rd, wr, hold=SHORT):
-        call("v", V.tensor_tensor, (out, in0, in1, op), rd, wr, hold)
+    def tt(out, in0, in1, op, rd, wr):
+        call("v", V.tensor_tensor, (out, in0, in1, op), rd, wr)
 
-    def turn(out, in_, rd, wr, hold=SHORT):
-        call("v", V.transpose, (out, in_), rd, wr, hold)
+    def turn(out, in_, rd, wr, **kw):
+        call("v", V.transpose, (out, in_), rd, wr, **kw)
 
     def scan(out, d0, d1, rd, wr):
         call("v", V.tensor_tensor_scan, (out, d0, d1, 0.0, A.mult, A.add), rd, wr)
 
     def quant(q, s, x, rd, wr):
-        call("v", V.quantize_mx, (q, s, x), rd, wr, 0.14)
+        call("v", V.quantize_mx, (q, s, x), rd, wr)
 
-    def product(b, stat, stat_s, mov, mov_s, rd):
-        call("p", P.matmul_mx, (bank(b), stat, stat_s, mov, mov_s, True, True), rd, [("ps", b)], 0.15)
+    def product(b, stat, stat_s, mov, mov_s, rd, name):
+        call("p", P.matmul_mx, (bank(b), stat, stat_s, mov, mov_s, True, True), rd, [("ps", b)], name=name)
 
-    def fill(ap, val, rd, key, hold=SHORT):
-        call("v", V.memset, (ap, val), rd, [key], hold)
+    def fill(ap, val, rd, key):
+        call("v", V.memset, (ap, val), rd, [key])
 
-    def iota(out, pattern, base, key, hold=0.17):
-        call("g", g.iota, (out, pattern, base, 0), [], [key], hold, allow_small_or_imprecise_dtypes=True)
+    def iota(out, pattern, base, key):
+        call("g", g.iota, (out, pattern, base, 0), [], [key], allow_small_or_imprecise_dtypes=True)
 
     def u8(ap):
         return ap.bitcast(dt.uint8)
@@ -164,95 +171,103 @@ def rank_program(g, core, T, topo):
     X = [T["xs%d" % t] for t in range(R + 1)]
     xk = lambda t, h: [("x", t, h, b) for b in range(4)]
 
-    dma("s", T.raw[:], T.ct[:], [], ["raw"], 1.1)
+    dma("s", T.raw[:], T.ct[:], [], ["raw"])
     dma("y", T.ut[:], T.u[:], [], ["ut"])
-    dma("s", X[0][:, 0:512], T.x[:, 0:512], [], xk(0, 0), 2.0)
-    dma("y", X[0][:, 512:1024], T.x[:, 512:1024], [], xk(0, 1), 2.4)
-    for h in range(2):
-        dma("y", X[0][:, 1024 + 512 * h:1536 + 512 * h], T.x[:, 512 * h:512 * h + 512], [], [("xd", 0, h)], 3.5)
+    dma("s", X[0][:, 0:512], T.x[:, 0:512], [], xk(0, 0))
+    dma("y", X[0][:, 512:1024], T.x[:, 512:1024], [], xk(0, 1))
     dma("y", u8(T.wq[:]), T.wc[:], [], ["wq"])
     dma("y", T.wp[:], T.ws[:], [], ["wp"])
-    dma("y", T.vt[:], T.v[:], [], ["vt"], 6.0)
+    dma("y", T.vt[:], T.v[:], [], ["vt"])
 
-    ucol, eps, p15, k16, is15, is1, dcon = range(0, 224, 32)
+    ucol, eps, k16, p15 = range(0, 128, 32)
     at = lambda c, p0=0, p1=128: T.kt[p0:p1, c:c + 1]
-    row16 = lambda p0=0, p1=128: T.kk[p0:p1, p15:p15 + 16]
+    row16 = lambda p0=0, p1=128, w=16: T.kk[p0:p1, p15:p15 + w]
+    one = lambda c, p0=0, p1=128: T.one[p0:p1, 8 * c:8 * c + 1]
     iota(T.kk[:, ucol:ucol + 32], [[0, 2], [16, 4], [1, 4]], 0, "k0")
+    iota(T.kk[:, p15:p15 + 48], [[0, 3], [1, 16]], 0, "k1")
     iota(T.row[:, 0:4], [[32, 4]], 0, "r0")
     iota(T.row[:, 4:8], [[0, 2], [64, 2]], 0, "r1")
-    iota(T.kk[:, p15:p15 + 32], [[0, 2], [1, 16]], 0, "k1")
-    iota(T.col[:], [[1, 256]], 0, "col", 0.6)
+    iota(T.kd[:], [[1, 256]], 0, "kd")
     iota(T.row[:, 16:32], [[64, 4], [16, 2], [0, 2]], 0, "r2")
-    iota(T.wj[:], [[1, 288]], -255, "wj", 0.7)
-    iota(T.wb[:, 256:512], [[1, 16], [16, 16]], 0, "wb1", 0.6)
-    fill(T.kk[:, eps:eps + 32], 0.0, [], "kz0")
-    fill(T.kk[:, k16:224], 0.0, [], "kz1", 0.12)
+    iota(T.wj[:], [[1, 288]], -255, "wj")
+    iota(T.wb[:, 256:512], [[1, 16], [16, 16]], 0, "wb1")
+    iota(T.col[:], [[1, 256]], 0, "col")
+    fill(T.kk[:, eps:eps + 48], 0.0, [], "kz")
+    fill(T.kk[:, k16 + 16:k16 + 32], 16.0, [], "k16")
     first = [(eps + 8, eps + 12, 80.0), (eps + 24, eps + 28, 80.0), (eps + 12, eps + 16, -48.0), (eps + 28, eps + 32, -48.0)]
     for i, (a, b, val) in enumerate(first):
-        fill(T.kk[:, a:b], val, ["kz0"], ("ke", i))
-    turn(T.kt[:, 0:64], T.kk[:, 0:64], ["k0", "kz0"] + [("ke", i) for i in range(4)], ["kt0"])
-    pieces = [(T.kk[:, k16 + 16:k16 + 32], 16.0), (T.kk[:, is15 + 15:is15 + 32:16], 1.0), (T.kk[:, is1 + 1:is1 + 32:16], 1.0),
-              (T.kk[64:128, dcon:dcon + 15], -16.0), (T.kk[64:128, dcon + 16:dcon + 31], -16.0), (T.kk[64:128, dcon + 15:dcon + 32:16], 240.0)]
-    for i, (ap, val) in enumerate(pieces):
-        fill(ap, val, ["kz1"], ("kp", i))
-    turn(T.kt[:, 64:224], T.kk[:, 64:224], ["k1", "kz1"] + [("kp", i) for i in range(len(pieces))], ["kt"], 0.15)
+        fill(T.kk[:, a:b], val, ["kz"], ("ke", i))
+    turn(T.kt[:], T.kk[:, 0:128], ["k0", "k1", "kz", "k16"] + [("ke", i) for i in range(4)], ["kt"])
     fill(T.dd[:], 2.0, [], "dd")
-    fill(T.dd[:, 0:128:8], 0.0, ["dd"], "dd0")
-    fill(T.dd[:, 4:128:8], 1.0 / 128, ["dd"], "dd4")
     fill(T.lt[:], 0, [], "ltz")
-    fill(T.one[0:96, 0:8], 1.0, [], "one0")
-    fill(T.one[96:128, 0:8], 16.0, [], "one1")
-    fill(T.one[:, 8:16], -TINY, [], "one2")
-    fill(T.ty[:, 32:48], 0.0, [], "tyz")
-    fill(T.tin[:], 0.0, [], "tinz")
-    ts(T.ucl[:, 0:1], at(ucol), at(eps), None, A.add, None, ["kt0"], ["uc0"])
-    ts(T.ucl[:, 1:8], T.row[:, 1:8], at(ucol), 127.0, A.add, A.min, ["kt0", "r0", "r1"], ["uc1"])
-    ts(T.km[64:128, :], row16(64), at(p15, 64), None, A.is_lt, None, ["kt"], ["km1"])
-    ts(T.km[0:64, :], row16(0, 64), at(k16, 0, 64), at(is1, 0, 64), A.add, A.mult, ["kt"], ["km0"])
+
+    def level(ap, w, val, rd, key, p0=0):
+        act(ap, T.kk[p0:128, 0:w], F.Identity, ["k0"] + rd, [key], scale=0.0, bias=val)
+    level(T.dd[:, 0:128:8], 16, 0.0, ["dd"], "dd0")
+    level(T.dd[:, 4:128:8], 16, 1.0 / 128, ["dd"], "dd4")
+    level(T.one[:, 0:16], 16, 1.0, [], "s01")
+    level(T.one[:, 16:24], 8, 0.0, [], "b0")
+    level(T.one[:, 24:32], 8, -TINY, [], "tiny")
+    level(T.one[96:128, 8:16], 8, 16.0, ["s01"], "s1", 96)
+    level(T.ty[:, 32:48], 16, 0.0, [], "tyz")
+    for i in range(2):
+        level(T.tin[:, 32 * i + 16:32 * i + 32], 16, 0.0, [], ("tinz", i))
+    ts(T.ucl[:, 0:1], at(ucol), at(eps), None, A.add, None, ["kt"], ["uc0"])
+    ts(T.ucl[:, 1:8], T.row[:, 1:8], at(ucol), 127.0, A.add, A.min, ["kt", "r0", "r1"], ["uc1"])
+    act(T.one[64:96, 0:16:8], T.kt[64:96, p15:p15 + 2], F.Relu, ["kt", "s01"], ["is15"], bias=-14.0)
+    act(one(2, 64, 96), one(0, 64, 96), F.Identity, ["is15", "b0"], ["b1"], scale=256.0, bias=-16.0)
+    ts(one(5), at(p15), 15.0, None, A.is_lt, None, ["kt"], ["not15"])
+    ts(T.km[64:128, :], row16(64, 128, 48), at(p15, 64), None, A.is_lt, None, ["kt"], ["km1"])
+    ts(T.km[0:64, :], row16(0, 64, 48), at(k16, 0, 64), one(5, 0, 64), A.add, A.mult, ["kt", "not15"], ["km0"])
     for i in range(2):
         ts(T.lt[0:64, 32 * i:32 * i + 16], row16(0, 64), 16.0, at(p15, 0, 64), A.mult, A.add, ["kt", "ltz"], [("ltj", i)])
-        act(T["k%d" % i][:], T.col[:], F.Identity, ["kt", "col"], [("kd", i)], 0.25, scale=at(is15), bias=at(dcon))
-    ts(T.one[:, 16:17], at(k16), 2.0, at(p15), A.mult, A.add, ["kt"], ["pj"])
-    ts(T.l7[:], T.row[:, 16:32], T.one[:, 16:17], None, A.add, None, ["pj", "r2"], [("l7", h, i) for h in range(2) for i in range(2)])
+    act(one(4), at(k16), F.Identity, ["kt"], ["pj"], scale=2.0, bias=at(p15))
+    ts(T.l7[:], T.row[:, 16:32], one(4), None, A.add, None, ["pj", "r2"], [("l7", h, i) for h in range(2) for i in range(2)], name="l7")
 
     for i in range(2):
         copy("v", T.tn[:, 16 * i:16 * i + 16], T.raw[:], ["raw"], [("tn", i)])
     turn(T.ty[:, 0:32], T.tn[:], [("tn", 0), ("tn", 1)], ["ty"])
-    moves = [(64, 0, 0, 0, 32), (96, 0, 0, 0, 32), (0, 16, 96, 16, 16), (64, 32, 32, 0, 32), (96, 32, 32, 0, 32), (96, 64, 96, 0, 16)]
-    for i, (p0, c0, p1, c1, w) in enumerate(moves):
-        copy("v", T.lt[p0:p0 + 32, c0:c0 + w], T.ty[p1:p1 + 32, c1:c1 + w], ["ty", "ltz"], [("lt", i)])
+    moves = [(64, 0, 0, 0, 32, 0.0), (96, 0, 0, 0, 32, 0.0), (0, 16, 96, 16, 16, 0.0), (64, 32, 32, 0, 32, 0.0), (96, 32, 32, 0, 32, 32.0),
+             (96, 64, 96, 0, 16, 0.0)]
+    for i, (p0, c0, p1, c1, w, shift) in enumerate(moves):
+        ts(T.lt[p0:p0 + 32, c0:c0 + w], T.ty[p1:p1 + 32, c1:c1 + w], shift, None, A.add, None, ["ty", "ltz"], [("lt", i)])
     for i, (c0, c1, w) in enumerate([(0, 0, 15), (16, 0, 15), (32, 16, 16), (48, 16, 16)]):
         tt(T.tz[96:128, c0:c0 + w], T.ty[64:96, c1:c1 + w], T.ty[64:96, c1 + 1:c1 + 1 + w], A.subtract, ["ty", "tyz"], [("tz", i)])
     ts(T.tz[96:128, 15:32:16], T.ty[64:96, 0:2], 0.0, T.ty[64:96, 15:16], A.mult, A.add, ["ty"], [("tz", 4)])
+    turn(T.kd[96:128, 0:64], T.tz[96:128, :], [("tz", k) for k in range(5)], ["kd"], name="kd3")
+    sk = ["kd", "is15", "b1", "s1"]
+    for i in range(4):
+        act(half(T.wm, i), T.km[:].indirect(lst(T.lt, 2 + i + 2 * (i // 2))), F.Copy,
+            [("lt", k) for k in ((0, 1, 2), (3, 4))[i // 2]] + ["km0", "km1"], [("wm", i)])
     for i in range(2):
-        turn(T["k%d" % i][96:128, 0:32], T.tz[96:128, 32 * i:32 * i + 32], [("tz", k) for k in ((0, 1, 4), (2, 3))[i]], [("kd", i)])
-        act(T.wm[:, 256 * i:256 * i + 256], T.km[:].indirect(T.lt[:, 32 * i + 16:32 * i + 32]), F.Copy,
-            [("lt", k) for k in ((0, 1, 2), (3, 4))[i]] + ["km0", "km1"], [("wm", i)], 2 * GATHER)
-    act(T.wd[:, 0:256], T.k0[:].indirect(T.lt[:, 0:16]), F.Copy, [("lt", 0), ("lt", 1), ("ltj", 0), ("kd", 0)], [("wd", 0)], 2 * GATHER)
-    act(T.wd[:, 256:512], T.k1[:].indirect(T.lt[:, 32:48]), F.Copy, [("lt", 3), ("lt", 4), ("ltj", 1), ("kd", 1), "one0", "one1"], [("wd", 1)],
-        2 * GATHER, scale=T.one[:, 0:1])
-    act(T.wb[:, 0:256], T.col[:].indirect(T.lt[:, 64:80]), F.Copy, [("lt", 5), "col"], ["wb0"], 2 * GATHER, scale=16.0)
+        ts(half(T.wd, i), T.kd[:].indirect(lst(T.lt, i)), one(0), one(2), A.mult, A.add, [("lt", 0), ("lt", 1), ("ltj", 0)] + sk, [("wd", i)])
+        act(half(T.wd, 2 + i), T.kd[:].indirect(lst(T.lt, 4 + i)), F.Identity, [("lt", 3), ("lt", 4), ("ltj", 1)] + sk, [("wd", 2 + i)],
+            scale=one(1), bias=one(2))
+        act(half(T.wb, i), row16().indirect(lst(T.lt, 8 + i)), F.Copy, [("lt", 5), "k1"], [("wb0", i)], scale=16.0)
 
     quant(T.qu[:], T.su[:], T.ut[:], ["ut"], ["qu"])
-    copy("v", u32(T.qup[:]), u32(T.qu[:]).indirect(T.ucl[:]), ["qu", "uc0", "uc1"], ["qup"], GATHER)
-    copy("s", T.sup[:], T.su[:].indirect(T.ucl[:]), ["qu", "uc0", "uc1"], ["sup"], GATHER)
-    quant(T.qv[:], T.sv[:], T.vt[:], ["vt"], ["qv"])
+    copy("v", u32(T.qup[:]), u32(T.qu[:]).indirect(T.ucl[:]), ["qu", "uc0", "uc1"], ["qup"])
+    copy("s", T.sup[:], T.su[:].indirect(T.ucl[:]), ["qu", "uc0", "uc1"], ["sup"])
 
     def state(t, h):
         if t:
-            for b in range(4):
+            for b in range(WIDE[t == R] if h == 0 else 0):
+                tt(X[t][:, b:1024:4], T.hh[:, 256 * b:256 * b + 256].indirect(T.lsib[:]), X[t - 1][:, b:1024:4], A.add,
+                   [("h", b, 0), ("h", b, 1), "lsib", ("x", t - 1, 0, b), ("x", t - 1, 1, b)], [("x", t, 0, b), ("x", t, 1, b)])
+            for b in range(WIDE[t == R], 4):
                 tt(half(X[t], h, b, 4, w=512), T.hh[:, 256 * b:256 * b + 256].indirect(lst(T.lsib, h)), half(X[t - 1], h, b, 4, w=512), A.add,
-                   [("h", b, 0), ("h", b, 1), "lsib", ("x", t - 1, h, b)], [("x", t, h, b)], GATHER)
-        if 0 < t < R:
-            call("g", g.affine_select, (half(X[t], h + 2, w=512), half(X[t], h, w=512), [[0, 512]], A.is_ge, 0.0, 0, 0),
-                 xk(t, h), [("xd", t, h)], 1.2)
+                   [("h", b, 0), ("h", b, 1), "lsib", ("x", t - 1, h, b)], [("x", t, h, b)])
+        for b in range(4 if t < R else 0):
+            call("g", g.affine_select, (half(T["xp%d" % t], 4 * b + h), half(X[t], h, b, 4, w=512), [[0, H]], A.is_ge, 0.0, 0, 0),
+                 [("x", t, h, b)], [("xp", t, h, b)])
+            dma("y", half(T["xp%d" % t], 4 * b + h + 2), half(T["xp%d" % t], 4 * b + h), [("xp", t, h, b)], [("xd", t, h, b)])
         qx, sx = half(T["qx%d" % t], h), half(T["sx%d" % t], h)
         quant(qx, sx, half(X[t], h, w=512), xk(t, h), [("qx", t, h)])
         stat, scale, keys = (T.qup, T.sup, ["qup", "sup"]) if t < R else (T.qv, T.sv, ["qv"])
-        product(h, stat[:], scale[:], qx, sx, keys + [("qx", t, h)])
+        product(h, stat[:], scale[:], qx, sx, keys + [("qx", t, h)], "score%d" % h)
 
     def places(t, h):
-        act(half(T.bits, h), bank(h), F.Sign, ["one2"], [("ps", h), ("bits", h)], 0.13, bias=T.one[:, 8:9])
+        act(half(T.bits, h), bank(h), F.Sign, ["tiny"], [("ps", h), ("bits", h)], bias=one(3))
         turn(half(T.bt, h), half(T.bits, h), [("bits", h)], [("bt", h)])
         scan(half(T.sc, h), T.dd[:], half(T.bt, h), [("bt", h), "dd0", "dd4"], [("sc", h)])
         for k, pos, q in (("d", 7, "s"), ("m", 15, "v")):
@@ -260,13 +275,13 @@ def rank_program(g, core, T, topo):
                 ts(lst(T["l" + k], h, 4 * i, end=4 * i + 4), half(T.sc, h, pos + 16 * i, 32), 8.0, 127.5 + 256 * i, A.mult, A.add,
                    [("sc", h)], [("l" + k, h, i)])
             copy(q, half(T["f" + k], h), T["w" + k][:].indirect(lst(T["l" + k], h)),
-                 [("l" + k, h, 0), ("l" + k, h, 1), ("w" + k, 0), ("w" + k, 1)], [("f" + k, h)], GATHER)
+                 [("l" + k, h, 0), ("l" + k, h, 1)] + [("w" + k, i) for i in range(4)], [("f" + k, h)])
             turn(half(T["t" + k], h), half(T["f" + k], h), [("f" + k, h)], [("t" + k, h)])
         scan(half(T.s2, h), half(T.tm, h), half(T.td, h), [("tm", h), ("td", h)], [("s2", h), ("a6", h)])
         for i in range(2):
-            ts(lst(T.l7, h, 4 * i + 1, 2, 96, end=4 * i + 4), half(T.tm, h, 32 * i + 1, 16, 0, 32, end=32 * i + 32), T.one[0:32, 16:17],
+            ts(lst(T.l7, h, 4 * i + 1, 2, 96, end=4 * i + 4), half(T.tm, h, 32 * i + 1, 16, 0, 32, end=32 * i + 32), one(4, 0, 32),
                128.0 * h + 64 * i, A.add, A.add, [("tm", h), "pj"], [("l7", h, i)])
-        copy("s", half(T.f7, h), T.wj[:].indirect(lst(T.l7, h)), [("l7", h, 0), ("l7", h, 1), "wj"], [("f7", h)], GATHER)
+        copy("s", half(T.f7, h), T.wj[:].indirect(lst(T.l7, h)), [("l7", h, 0), ("l7", h, 1), "wj"], [("f7", h)])
         six = half(T.s2, h, 15, 16, 96, end=64)
         tt(six, six, half(T.s2, h, 79, 16, 96), A.add, [("s2", h)], [("a6", h)])
         ts(lst(T.l3, h, 1, 2, 0, 96), half(T.s2, h, 79, 16, 0, 96), 256.0, None, A.add, None, [("s2", h)], [("l3", h, 2)])
@@ -274,33 +289,32 @@ def rank_program(g, core, T, topo):
             ts(lst(T.l3, h, i, 2, 96 * i), half(T.s2, h, 15, 16, 96 * i, end=64), 256.0 * (1 - i), None, A.add, None,
                [("s2", h), ("a6", h)], [("l3", h, i)])
         tt(half(T.f3, h), T.wb[:].indirect(lst(T.l3, h)), half(T.f7, h), A.add,
-           [("l3", h, k) for k in range(3)] + [("f7", h), "wb0", "wb1"], [("f3", h)], GATHER)
+           [("l3", h, k) for k in range(3)] + [("f7", h), ("wb0", 0), ("wb0", 1), "wb1"], [("f3", h)])
         turn(half(T.t3, h), half(T.f3, h), [("f3", h)], [("t3", h)])
 
     mymask = engines_of(rank)
 
     def send(t, h):
-        for e in (2, 3, 0, 1):
-            ts(lst(T.lz, 2 * e + h), half(T.t3, h, 0, 16), 4.0, 1020.0 + e, A.mult, A.add, [("t3", h)], [("lz", e, h)])
-            copy(PICKS[h][e], half(T["zz%d" % t], h, e, 4, w=512), X[t][:, 0:1536 + 512 * h].indirect(lst(T.lz, 2 * e + h)),
-                 xk(t, 0) + xk(t, 1) + [("xd", t, k) for k in range(h + 1)] + [("lz", e, h)], [("z", t, e, h)], GATHER)
+        ts(lst(T.lz, h), half(T.t3, h, 0, 16), 255.0, None, A.add, None, [("t3", h)], [("lz", h)])
+        for e in range(4):
+            copy(PICKS[h][e], half(T["zz%d" % t], h, e, 4, w=512), T["xp%d" % t][:, 512 * e:512 * e + 384 + H * h].indirect(lst(T.lz, h)),
+                 [("xp", t, k, e) for k in range(2)] + [("xd", t, k, e) for k in range(h + 1)] + [("lz", h)], [("z", t, e, h)])
         qz, sz = half(T["qz%d" % t], h), half(T["sz%d" % t], h)
         quant(qz, sz, half(T["zz%d" % t], h, w=512), [("z", t, e, h) for e in range(4)], [("qz", t, h)])
         rid, pid, _ = topo.addr(cores[(rank + 1 + t) % n])
         for i, (dst, src) in enumerate(((u8(half(T["lq%d" % t], h)), u8(qz)), (half(T["ls%d" % t], h), sz))):
-            call("g", g.remote_dma, (dst, src, T.sem["arr%d%d" % (t, h)], T.sem.sent, pid, rid, mymask), [("qz", t, h)], [("far", t, h, i)],
-                 0.2, FAR + (1 - h), "remote")
+            call("g", g.remote_dma, (dst, src, T.sem["arr%d%d" % (t, h)], T.sem.sent, pid, rid, mymask), [("qz", t, h)], [("far", t, h, i)], "remote")
 
     def layer(t, h):
-        call("p", None, ("arr%d%d" % (t, h), NCALL * ones(engines_of((rank - 1 - t) % n))), [], [("lq", t, h)], 0.0, 0.0, "arrive",
-             after=[("far", t, h, i) for i in range(NCALL)])
+        call("p", None, ("arr%d%d" % (t, h), NCALL * ones(engines_of((rank - 1 - t) % n))), [("far", t, h, i) for i in range(NCALL)],
+             [("lq", t, h)], "arrive")
         for b in range(4):
             k = 4 * h + b
-            product(k, half(T.wq, b), half(T.wp, b), half(T["lq%d" % t], h), half(T["ls%d" % t], h), ["wq", "wp", ("lq", t, h)])
+            product(k, half(T.wq, b), half(T.wp, b), half(T["lq%d" % t], h), half(T["ls%d" % t], h), ["wq", "wp", ("lq", t, h)], "layer%d" % k)
             if h == 1 and b == 0:
-                ts(half(T.hh, 2 * b + h), bank(k), 0.03125, None, A.mult, None, [], [("ps", k), ("h", b, h)], 0.13)
+                ts(half(T.hh, 2 * b + h), bank(k), 0.03125, None, A.mult, None, [], [("ps", k), ("h", b, h)])
             else:
-                act(half(T.hh, 2 * b + h), bank(k), F.Copy, [], [("ps", k), ("h", b, h)], 0.13, scale=0.03125)
+                act(half(T.hh, 2 * b + h), bank(k), F.Copy, [], [("ps", k), ("h", b, h)], scale=0.03125)
 
     def sibling(t):
         for i, k in enumerate((0, 2, 1, 3)):
@@ -309,33 +323,37 @@ def rank_program(g, core, T, topo):
         ts(T.wa[:, 0:16], T.wi[:], 223, None, A.bitwise_and, None, wik, ["wa0"])
         ts(T.wa[:, 16:32], T.wi[:], 16, None, A.bitwise_and, None, wik, ["wa1"])
         ts(T.wa[:, 32:48], T.wi[:], 1, 16, A.logical_shift_right, A.bitwise_and, wik, ["wa2"])
-        tt(T.tin[:, 0:16], T.wa[:, 0:16], T.wa[:, 16:32], A.add, ["wa0", "wa1", "tinz"], ["tin0"])
-        copy("v", T.tin[:, 32:48], T.wa[:, 32:48], ["wa2", "tinz"], ["tin1"])
-        turn(T.y1[:], T.tin[:], ["tin0", "tin1"], ["y1"])
+        if t == R - 1:
+            ts(T.wa[:, 48:64], T.wi[:], 255, None, A.bitwise_and, None, wik, ["wa3"])
+        tt(T.tin[:, 0:16], T.wa[:, 0:16], T.wa[:, 16:32], A.add, ["wa0", "wa1"], ["tin0"])
+        copy("v", T.tin[:, 32:48], T.wa[:, 32:48], ["wa2"], ["tin1"])
+        if t == R - 1:
+            copy("v", T.lown[:], T.wa[:, 48:64], ["wa3"], ["lown"])
+            copy("s", T.lof[:], T.col[:].indirect(T.lown[:]), ["lown", "col"], ["lof"])
+            dma("y", T.lo[:], T.lof[0:128:16, :], ["lof"], ["lo"])
+        turn(T.y1[:], T.tin[:], ["tin0", "tin1", ("tinz", 0), ("tinz", 1)], ["y1"])
         for i in range(2):
             tt(T.y2[:, 16 * i:16 * i + 16], T.y1[:, 16 - 16 * i:32 - 16 * i], T.y1[:, 48 - 16 * i:64 - 16 * i], A.add, ["y1"], [("y2", i)])
         turn(T.y3[:], T.y2[:], [("y2", 0), ("y2", 1)], ["y3"])
         copy("v", T.lsib[:], T.y3[:, 0:16], ["y3"], ["lsib"])
-        if t == R - 1:
-            ts(T.wa[:, 48:64], T.wi[:], 255, None, A.bitwise_and, None, wik, ["wa3"])
-            copy("v", T.lown[:], T.wa[:, 48:64], ["wa3"], ["lown"])
-            copy("s", T.lof[:], T.col[:].indirect(T.lown[:]), ["lown", "col"], ["lof"], 2 * GATHER)
-            dma("y", T.lo[:], T.lof[0:128:16, :], ["lof"], ["lo"])
 
     for t in range(R):
         for step in (state, places, send):
             for h in range(2):
                 step(t, h)
+        if t == 0:
+            quant(T.qv[:], T.sv[:], T.vt[:], ["vt"], ["qv"])
         sibling(t)
         for h in range(2):
             layer(t, h)
+        phase[0] += 1
 
     qx, sx = T["qx%d" % R], T["sx%d" % R]
     for h in range(2):
         state(R, h)
         dma("y", half(T.oc, h, w=512), u8(half(qx, h)), [("qx", R, h)], [("oc", h)])
-        copy("sv"[h], half(T.yo, h), bank(h), [], [("ps", h), ("yo", h)], 0.13)
-        dma("s", half(T.y, h), half(T.yo, h), [("yo", h)], [("y", h)])
+        copy("v", half(T.yo, h), bank(h), [], [("ps", h), ("yo", h)])
+        dma("sy"[h], half(T.y, h), half(T.yo, h), [("yo", h)], [("y", h)])
     for k in range(4):
         dma("sy"[k % 2], T.osc[4 * k:4 * k + 4, :], sx[32 * k:32 * k + 4, :], [("qx", R, 0), ("qx", R, 1)], [("osc", k)])
 

from concourse.mybir import dt, AluOpType, ActivationFunctionType

C = 256
H = C // 2
R = 3
X4 = "float8_e4m3fn_x4"
TINY = 1e-35
SCRATCH = {
    "ut": ("sbuf", [128, 512], "bfloat16"), "vt": ("sbuf", [128, 512], "bfloat16"),
    "qu": ("sbuf", [128, 128], X4), "su": ("sbuf", [128, 128], "uint8"),
    "qup": ("sbuf", [128, 128], X4), "sup": ("sbuf", [128, 128], "uint8"),
    "qv": ("sbuf", [128, 128], X4), "sv": ("sbuf", [128, 128], "uint8"),
    "wq": ("sbuf", [128, 512], X4), "wp": ("sbuf", [128, 512], "uint8"),
    "ps": ("psum", [128, 4096], "float32"),
    "kk": ("sbuf", [128, 144], "float32"), "kt": ("sbuf", [128, 128], "float32"), "row": ("sbuf", [128, 32], "float32"),
    "col": ("sbuf", [128, 256], "bfloat16"), "one": ("sbuf", [128, 48], "float32"), "ucl": ("sbuf", [128, 8], "uint16"),
    "raw": ("sbuf", [128, 16], "int32"), "tn": ("sbuf", [128, 32], "bfloat16"), "ty": ("sbuf", [128, 48], "bfloat16"),
    "tz": ("sbuf", [128, 64], "bfloat16"), "lt": ("sbuf", [128, 80], "uint16"),
    "kd": ("sbuf", [128, 256], "bfloat16"), "km": ("sbuf", [128, 48], "bfloat16"),
    "wd": ("sbuf", [128, 512], "bfloat16"), "wm": ("sbuf", [128, 512], "bfloat16"), "wb": ("sbuf", [128, 512], "bfloat16"),
    "wj": ("sbuf", [128, 288], "bfloat16"), "dd": ("sbuf", [128, 128], "bfloat16"),
    "bits": ("sbuf", [128, 256], "bfloat16"), "bt": ("sbuf", [128, 256], "bfloat16"), "sc": ("sbuf", [128, 256], "bfloat16"),
    "ld": ("sbuf", [128, 16], "uint16"), "lm": ("sbuf", [128, 16], "uint16"), "l3": ("sbuf", [128, 16], "uint16"),
    "l7": ("sbuf", [128, 16], "uint16"), "lz": ("sbuf", [128, 16], "uint16"),
    "fd": ("sbuf", [128, 256], "bfloat16"), "fm": ("sbuf", [128, 256], "bfloat16"), "f3": ("sbuf", [128, 256], "bfloat16"),
    "td": ("sbuf", [128, 256], "bfloat16"), "tm": ("sbuf", [128, 256], "bfloat16"), "t3": ("sbuf", [128, 256], "bfloat16"),
    "f7": ("sbuf", [128, 256], "bfloat16"), "s2": ("sbuf", [128, 256], "bfloat16"),
    "wi": ("sbuf", [128, 16], "int32"), "wa": ("sbuf", [128, 64], "int32"),
    "tin": ("sbuf", [128, 64], "bfloat16"), "y1": ("sbuf", [128, 64], "bfloat16"),
    "y2": ("sbuf", [128, 32], "bfloat16"), "y3": ("sbuf", [128, 32], "bfloat16"),
    "lsib": ("sbuf", [128, 16], "uint16"), "lown": ("sbuf", [128, 16], "uint16"), "lof": ("sbuf", [128, 256], "float32"),
    "hh": ("sbuf", [128, 1024], "float32"), "yo": ("sbuf", [128, 256], "float32"),
}
for _t in range(R + 1):
    SCRATCH["xs%d" % _t] = ("sbuf", [128, 1024], "bfloat16")
    SCRATCH["qx%d" % _t] = ("sbuf", [128, C], X4)
    SCRATCH["sx%d" % _t] = ("sbuf", [128, C], "uint8")
for _t in range(R):
    SCRATCH["xp%d" % _t] = ("sbuf", [128, 2048], "bfloat16")
    SCRATCH["zz%d" % _t] = ("sbuf", [128, 1024], "bfloat16")
    SCRATCH["qz%d" % _t] = ("sbuf", [128, C], X4)
    SCRATCH["sz%d" % _t] = ("sbuf", [128, C], "uint8")
    SCRATCH["lq%d" % _t] = ("sbuf", [128, C], X4)
    SCRATCH["ls%d" % _t] = ("sbuf", [128, C], "uint8")

NDMA = 44
NCALL = 2
SEMAPHORES = (["cv", "cs", "cp", "cg", "sent"] + ["arr%d%d" % (_t, _h) for _t in range(R) for _h in range(2)]
              + ["d%d" % _i for _i in range(NDMA)])

A = AluOpType
F = ActivationFunctionType

PICKS = ("vvss", "vvss")
WIDE = (0, 3)

ORDER = {
    (0, "v"): "kz dd ltz k16 ke0 ke1 ke2 ke3 kt not15 km1 uc0 uc1 tn0 tn1 ltj0 ltj1 km0 ty l7 qu lt0 lt1 lt2 qup qx0 lt3 lt4 tz0 tz1 tz2 tz3 tz4 "
              "qx1 kd3 lt5 bt0 wd0 sc0 wd1 lm00 lm01 ld00 ld01 bt1 fm0 sc1 tm0 td0 ld10 ld11 lm10 s20 lm11 l700 l701 a60 fm1 l302 l300 l301 "
              "tm1 td1 f30 l710 s21 l711 t30 a61 lz0 l312 l310 l311 z00 z10 f31 qz0 t31 lz1 wi0 wi1 z01 wi2 z11 wi3 qz1",
    (0, "s"): "raw x00 b0 s01 tiny tyz dd0 is15 pj dd4 s1 b1 tinz0 tinz1 sup wm0 wm1 wm2 bits0 wm3 wd3 bits1 wd2 fd0 wb00 wb01 fd1 f70 f71 z20 z30 z21 z31",
    (0, "g"): "k0 k1 r0 r1 r2 kd wb1 wj xp00 xp01 xp02 xp03 xp10 xp11 xp12 xp13 col",
    (1, "v"): "x00 x01 x02 x03 x10 qx0 x11 x12 x13 qx1 bt0 sc0 ld00 ld01 lm00 lm01 bt1 fm0 sc1 td0 tm0 lm10 lm11 ld10 ld11 l700 s20 fm1 l701 "
              "a60 l302 tm1 td1 l300 l301 l710 s21 l711 f30 a61 l312 t30 l310 l311 lz0 f31 z00 t31 z10 lz1 qz0 z01 z11 wi0 wi1 qz1 wi2 wi3",
    (1, "s"): "bits0 bits1 fd0 fd1 f70 f71 z20 z30 z21 z31",
    (3, "v"): "x00 x01 x02 x03 x13 qx0 qx1 yo0 yo1",
    (3, "s"): "osc0 osc2 y0",
    (3, "y"): "oc0 oc1 osc1 osc3 y1",
}


def in_order(calls):
    before, wrote, readers = [], {}, {}
    for i, c in enumerate(calls):
        before.append({wrote[k] for k in c["rd"] + c["wr"] if k in wrote} | {r for k in c["wr"] for r in readers.get(k, [])})
        for k in c["rd"]:
            readers.setdefault(k, []).append(i)
        for k in c["wr"]:
            wrote[k], readers[k] = i, []

    def place(i):
        c = calls[i]
        names = ORDER.get((c["phase"] if c["phase"] in (0, R) else 1, c["q"]), "").split()
        return c["phase"], names.index(c["name"]) if c["name"] in names else len(names), i
    queues = {q: sorted((i for i, c in enumerate(calls) if c["q"] == q), key=place) for q in "ysgvp"}
    row, out = [], set()
    while len(row) < len(calls):
        i = next(v[0] for v in queues.values() if v and before[v[0]] <= out)
        queues[calls[i]["q"]].pop(0)
        row.append(calls[i])
        out.add(i)
    return row


def rank_program(g, core, T, topo):
    rank = T.rank_of(core)
    if rank is None:
        return
    cores = T.cores
    n = len(cores)
    V, S, P = g.vector, g.scalar, g.tensor
    Q = {"v": V, "s": S, "p": P, "g": g, "y": g.sync}
    calls, phase = [], [0]

    def call(q, fn, args, rd, wr, kind="compute", name=None, **kw):
        key = ([k for k in wr if k[0] != "ps"] + wr)[0]
        if not isinstance(key, str):
            key = key[0] + "".join(str(k) for k in key[1 + (key[0] in ("x", "xp", "xd", "qx", "z", "qz", "far", "lq")):])
        calls.append(dict(name=name or key, phase=phase[0], q=q, fn=fn, args=args, kw=kw, rd=list(rd), wr=list(wr), kind=kind))

    def dma(q, out, in_, rd, wr):
        call(q, Q[q].dma_start, (out, in_), rd, wr, "dma")

    def act(out, in_, func, rd, wr, **kw):
        call("s", S.activation, (out, in_, func), rd, wr, **kw)

    def copy(q, out, in_, rd, wr):
        if q == "v":
            call("v", V.tensor_copy, (out, in_), rd, wr)
        else:
            act(out, in_, F.Copy, rd, wr)

    def ts(out, in0, s1, s2, op0, op1, rd, wr, **kw):
        call("v", V.tensor_scalar, (out, in0, s1, s2, op0) + ((op1,) if op1 is not None else ()), rd, wr, **kw)

    def tt(out, in0, in1, op, rd, wr):
        call("v", V.tensor_tensor, (out, in0, in1, op), rd, wr)

    def turn(out, in_, rd, wr, **kw):
        call("v", V.transpose, (out, in_), rd, wr, **kw)

    def scan(out, d0, d1, rd, wr):
        call("v", V.tensor_tensor_scan, (out, d0, d1, 0.0, A.mult, A.add), rd, wr)

    def quant(q, s, x, rd, wr):
        call("v", V.quantize_mx, (q, s, x), rd, wr)

    def product(b, stat, stat_s, mov, mov_s, rd, name):
        call("p", P.matmul_mx, (bank(b), stat, stat_s, mov, mov_s, True, True), rd, [("ps", b)], name=name)

    def fill(ap, val, rd, key):
        call("v", V.memset, (ap, val), rd, [key])

    def iota(out, pattern, base, key):
        call("g", g.iota, (out, pattern, base, 0), [], [key], allow_small_or_imprecise_dtypes=True)

    def u8(ap):
        return ap.bitcast(dt.uint8)

    def u32(ap):
        return ap.bitcast(dt.uint32)

    def bank(b):
        return T.ps[:, 512 * b:512 * b + H]

    def engines_of(r):
        m = -1
        for t in range(R):
            m &= topo.mask(cores[r], cores[(r + 1 + t) % n])
        return m

    def ones(m):
        return bin(m).count("1")

    def half(buf, h, a=0, step=1, p0=0, p1=128, w=H, end=None):
        return buf[p0:p1, w * h + a:w * h + (w if end is None else end):step]

    def lst(buf, h, a=0, step=1, p0=0, p1=128, end=None):
        return half(buf, h, a, step, p0, p1, 8, end)

    X = [T["xs%d" % t] for t in range(R + 1)]
    xk = lambda t, h: [("x", t, h, b) for b in range(4)]

    dma("s", T.raw[:], T.ct[:], [], ["raw"])
    dma("y", T.ut[:], T.u[:], [], ["ut"])
    dma("s", X[0][:, 0:512], T.x[:, 0:512], [], xk(0, 0))
    dma("y", X[0][:, 512:1024], T.x[:, 512:1024], [], xk(0, 1))
    dma("y", u8(T.wq[:]), T.wc[:], [], ["wq"])
    dma("y", T.wp[:], T.ws[:], [], ["wp"])
    dma("y", T.vt[:], T.v[:], [], ["vt"])

    ucol, eps, k16, p15 = range(0, 128, 32)
    at = lambda c, p0=0, p1=128: T.kt[p0:p1, c:c + 1]
    row16 = lambda p0=0, p1=128, w=16: T.kk[p0:p1, p15:p15 + w]
    one = lambda c, p0=0, p1=128: T.one[p0:p1, 8 * c:8 * c + 1]
    iota(T.kk[:, ucol:ucol + 32], [[0, 2], [16, 4], [1, 4]], 0, "k0")
    iota(T.kk[:, p15:p15 + 48], [[0, 3], [1, 16]], 0, "k1")
    iota(T.row[:, 0:4], [[32, 4]], 0, "r0")
    iota(T.row[:, 4:8], [[0, 2], [64, 2]], 0, "r1")
    iota(T.kd[:], [[1, 256]], 0, "kd")
    iota(T.row[:, 16:32], [[64, 4], [16, 2], [0, 2]], 0, "r2")
    iota(T.wj[:], [[1, 288]], -255, "wj")
    iota(T.wb[:, 256:512], [[1, 16], [16, 16]], 0, "wb1")
    iota(T.col[:], [[1, 256]], 0, "col")
    fill(T.kk[:, eps:eps + 48], 0.0, [], "kz")
    fill(T.kk[:, k16 + 16:k16 + 32], 16.0, [], "k16")
    first = [(eps + 8, eps + 12, 80.0), (eps + 24, eps + 28, 80.0), (eps + 12, eps + 16, -48.0), (eps + 28, eps + 32, -48.0)]
    for i, (a, b, val) in enumerate(first):
        fill(T.kk[:, a:b], val, ["kz"], ("ke", i))
    turn(T.kt[:], T.kk[:, 0:128], ["k0", "k1", "kz", "k16"] + [("ke", i) for i in range(4)], ["kt"])
    fill(T.dd[:], 2.0, [], "dd")
    fill(T.lt[:], 0, [], "ltz")

    def level(ap, w, val, rd, key, p0=0):
        act(ap, T.kk[p0:128, 0:w], F.Identity, ["k0"] + rd, [key], scale=0.0, bias=val)
    level(T.dd[:, 0:128:8], 16, 0.0, ["dd"], "dd0")
    level(T.dd[:, 4:128:8], 16, 1.0 / 128, ["dd"], "dd4")
    level(T.one[:, 0:16], 16, 1.0, [], "s01")
    level(T.one[:, 16:24], 8, 0.0, [], "b0")
    level(T.one[:, 24:32], 8, -TINY, [], "tiny")
    level(T.one[96:128, 8:16], 8, 16.0, ["s01"], "s1", 96)
    level(T.ty[:, 32:48], 16, 0.0, [], "tyz")
    for i in range(2):
        level(T.tin[:, 32 * i + 16:32 * i + 32], 16, 0.0, [], ("tinz", i))
    ts(T.ucl[:, 0:1], at(ucol), at(eps), None, A.add, None, ["kt"], ["uc0"])
    ts(T.ucl[:, 1:8], T.row[:, 1:8], at(ucol), 127.0, A.add, A.min, ["kt", "r0", "r1"], ["uc1"])
    act(T.one[64:96, 0:16:8], T.kt[64:96, p15:p15 + 2], F.Relu, ["kt", "s01"], ["is15"], bias=-14.0)
    act(one(2, 64, 96), one(0, 64, 96), F.Identity, ["is15", "b0"], ["b1"], scale=256.0, bias=-16.0)
    ts(one(5), at(p15), 15.0, None, A.is_lt, None, ["kt"], ["not15"])
    ts(T.km[64:128, :], row16(64, 128, 48), at(p15, 64), None, A.is_lt, None, ["kt"], ["km1"])
    ts(T.km[0:64, :], row16(0, 64, 48), at(k16, 0, 64), one(5, 0, 64), A.add, A.mult, ["kt", "not15"], ["km0"])
    for i in range(2):
        ts(T.lt[0:64, 32 * i:32 * i + 16], row16(0, 64), 16.0, at(p15, 0, 64), A.mult, A.add, ["kt", "ltz"], [("ltj", i)])
    act(one(4), at(k16), F.Identity, ["kt"], ["pj"], scale=2.0, bias=at(p15))
    ts(T.l7[:], T.row[:, 16:32], one(4), None, A.add, None, ["pj", "r2"], [("l7", h, i) for h in range(2) for i in range(2)], name="l7")

    for i in range(2):
        copy("v", T.tn[:, 16 * i:16 * i + 16], T.raw[:], ["raw"], [("tn", i)])
    turn(T.ty[:, 0:32], T.tn[:], [("tn", 0), ("tn", 1)], ["ty"])
    moves = [(64, 0, 0, 0, 32, 0.0), (96, 0, 0, 0, 32, 0.0), (0, 16, 96, 16, 16, 0.0), (64, 32, 32, 0, 32, 0.0), (96, 32, 32, 0, 32, 32.0),
             (96, 64, 96, 0, 16, 0.0)]
    for i, (p0, c0, p1, c1, w, shift) in enumerate(moves):
        ts(T.lt[p0:p0 + 32, c0:c0 + w], T.ty[p1:p1 + 32, c1:c1 + w], shift, None, A.add, None, ["ty", "ltz"], [("lt", i)])
    for i, (c0, c1, w) in enumerate([(0, 0, 15), (16, 0, 15), (32, 16, 16), (48, 16, 16)]):
        tt(T.tz[96:128, c0:c0 + w], T.ty[64:96, c1:c1 + w], T.ty[64:96, c1 + 1:c1 + 1 + w], A.subtract, ["ty", "tyz"], [("tz", i)])
    ts(T.tz[96:128, 15:32:16], T.ty[64:96, 0:2], 0.0, T.ty[64:96, 15:16], A.mult, A.add, ["ty"], [("tz", 4)])
    turn(T.kd[96:128, 0:64], T.tz[96:128, :], [("tz", k) for k in range(5)], ["kd"], name="kd3")
    sk = ["kd", "is15", "b1", "s1"]
    for i in range(4):
        act(half(T.wm, i), T.km[:].indirect(lst(T.lt, 2 + i + 2 * (i // 2))), F.Copy,
            [("lt", k) for k in ((0, 1, 2), (3, 4))[i // 2]] + ["km0", "km1"], [("wm", i)])
    for i in range(2):
        ts(half(T.wd, i), T.kd[:].indirect(lst(T.lt, i)), one(0), one(2), A.mult, A.add, [("lt", 0), ("lt", 1), ("ltj", 0)] + sk, [("wd", i)])
        act(half(T.wd, 2 + i), T.kd[:].indirect(lst(T.lt, 4 + i)), F.Identity, [("lt", 3), ("lt", 4), ("ltj", 1)] + sk, [("wd", 2 + i)],
            scale=one(1), bias=one(2))
        act(half(T.wb, i), row16().indirect(lst(T.lt, 8 + i)), F.Copy, [("lt", 5), "k1"], [("wb0", i)], scale=16.0)

    quant(T.qu[:], T.su[:], T.ut[:], ["ut"], ["qu"])
    copy("v", u32(T.qup[:]), u32(T.qu[:]).indirect(T.ucl[:]), ["qu", "uc0", "uc1"], ["qup"])
    copy("s", T.sup[:], T.su[:].indirect(T.ucl[:]), ["qu", "uc0", "uc1"], ["sup"])

    def state(t, h):
        if t:
            for b in range(WIDE[t == R] if h == 0 else 0):
                tt(X[t][:, b:1024:4], T.hh[:, 256 * b:256 * b + 256].indirect(T.lsib[:]), X[t - 1][:, b:1024:4], A.add,
                   [("h", b, 0), ("h", b, 1), "lsib", ("x", t - 1, 0, b), ("x", t - 1, 1, b)], [("x", t, 0, b), ("x", t, 1, b)])
            for b in range(WIDE[t == R], 4):
                tt(half(X[t], h, b, 4, w=512), T.hh[:, 256 * b:256 * b + 256].indirect(lst(T.lsib, h)), half(X[t - 1], h, b, 4, w=512), A.add,
                   [("h", b, 0), ("h", b, 1), "lsib", ("x", t - 1, h, b)], [("x", t, h, b)])
        for b in range(4 if t < R else 0):
            call("g", g.affine_select, (half(T["xp%d" % t], 4 * b + h), half(X[t], h, b, 4, w=512), [[0, H]], A.is_ge, 0.0, 0, 0),
                 [("x", t, h, b)], [("xp", t, h, b)])
            dma("y", half(T["xp%d" % t], 4 * b + h + 2), half(T["xp%d" % t], 4 * b + h), [("xp", t, h, b)], [("xd", t, h, b)])
        qx, sx = half(T["qx%d" % t], h), half(T["sx%d" % t], h)
        quant(qx, sx, half(X[t], h, w=512), xk(t, h), [("qx", t, h)])
        stat, scale, keys = (T.qup, T.sup, ["qup", "sup"]) if t < R else (T.qv, T.sv, ["qv"])
        product(h, stat[:], scale[:], qx, sx, keys + [("qx", t, h)], "score%d" % h)

    def places(t, h):
        act(half(T.bits, h), bank(h), F.Sign, ["tiny"], [("ps", h), ("bits", h)], bias=one(3))
        turn(half(T.bt, h), half(T.bits, h), [("bits", h)], [("bt", h)])
        scan(half(T.sc, h), T.dd[:], half(T.bt, h), [("bt", h), "dd0", "dd4"], [("sc", h)])
        for k, pos, q in (("d", 7, "s"), ("m", 15, "v")):
            for i in range(2):
                ts(lst(T["l" + k], h, 4 * i, end=4 * i + 4), half(T.sc, h, pos + 16 * i, 32), 8.0, 127.5 + 256 * i, A.mult, A.add,
                   [("sc", h)], [("l" + k, h, i)])
            copy(q, half(T["f" + k], h), T["w" + k][:].indirect(lst(T["l" + k], h)),
                 [("l" + k, h, 0), ("l" + k, h, 1)] + [("w" + k, i) for i in range(4)], [("f" + k, h)])
            turn(half(T["t" + k], h), half(T["f" + k], h), [("f" + k, h)], [("t" + k, h)])
        scan(half(T.s2, h), half(T.tm, h), half(T.td, h), [("tm", h), ("td", h)], [("s2", h), ("a6", h)])
        for i in range(2):
            ts(lst(T.l7, h, 4 * i + 1, 2, 96, end=4 * i + 4), half(T.tm, h, 32 * i + 1, 16, 0, 32, end=32 * i + 32), one(4, 0, 32),
               128.0 * h + 64 * i, A.add, A.add, [("tm", h), "pj"], [("l7", h, i)])
        copy("s", half(T.f7, h), T.wj[:].indirect(lst(T.l7, h)), [("l7", h, 0), ("l7", h, 1), "wj"], [("f7", h)])
        six = half(T.s2, h, 15, 16, 96, end=64)
        tt(six, six, half(T.s2, h, 79, 16, 96), A.add, [("s2", h)], [("a6", h)])
        ts(lst(T.l3, h, 1, 2, 0, 96), half(T.s2, h, 79, 16, 0, 96), 256.0, None, A.add, None, [("s2", h)], [("l3", h, 2)])
        for i in range(2):
            ts(lst(T.l3, h, i, 2, 96 * i), half(T.s2, h, 15, 16, 96 * i, end=64), 256.0 * (1 - i), None, A.add, None,
               [("s2", h), ("a6", h)], [("l3", h, i)])
        tt(half(T.f3, h), T.wb[:].indirect(lst(T.l3, h)), half(T.f7, h), A.add,
           [("l3", h, k) for k in range(3)] + [("f7", h), ("wb0", 0), ("wb0", 1), "wb1"], [("f3", h)])
        turn(half(T.t3, h), half(T.f3, h), [("f3", h)], [("t3", h)])

    mymask = engines_of(rank)

    def send(t, h):
        ts(lst(T.lz, h), half(T.t3, h, 0, 16), 255.0, None, A.add, None, [("t3", h)], [("lz", h)])
        for e in range(4):
            copy(PICKS[h][e], half(T["zz%d" % t], h, e, 4, w=512), T["xp%d" % t][:, 512 * e:512 * e + 384 + H * h].indirect(lst(T.lz, h)),
                 [("xp", t, k, e) for k in range(2)] + [("xd", t, k, e) for k in range(h + 1)] + [("lz", h)], [("z", t, e, h)])
        qz, sz = half(T["qz%d" % t], h), half(T["sz%d" % t], h)
        quant(qz, sz, half(T["zz%d" % t], h, w=512), [("z", t, e, h) for e in range(4)], [("qz", t, h)])
        rid, pid, _ = topo.addr(cores[(rank + 1 + t) % n])
        for i, (dst, src) in enumerate(((u8(half(T["lq%d" % t], h)), u8(qz)), (half(T["ls%d" % t], h), sz))):
            call("g", g.remote_dma, (dst, src, T.sem["arr%d%d" % (t, h)], T.sem.sent, pid, rid, mymask), [("qz", t, h)], [("far", t, h, i)], "remote")

    def layer(t, h):
        call("p", None, ("arr%d%d" % (t, h), NCALL * ones(engines_of((rank - 1 - t) % n))), [("far", t, h, i) for i in range(NCALL)],
             [("lq", t, h)], "arrive")
        for b in range(4):
            k = 4 * h + b
            product(k, half(T.wq, b), half(T.wp, b), half(T["lq%d" % t], h), half(T["ls%d" % t], h), ["wq", "wp", ("lq", t, h)], "layer%d" % k)
            if h == 1 and b == 0:
                ts(half(T.hh, 2 * b + h), bank(k), 0.03125, None, A.mult, None, [], [("ps", k), ("h", b, h)])
            else:
                act(half(T.hh, 2 * b + h), bank(k), F.Copy, [], [("ps", k), ("h", b, h)], scale=0.03125)

    def sibling(t):
        for i, k in enumerate((0, 2, 1, 3)):
            ts(T.wi[:, i:16:4], T.t3[:, 16 * k:256:64], 255.0, None, A.add, None, [("t3", 0), ("t3", 1)], [("wi", i)])
        wik = [("wi", i) for i in range(4)]
        ts(T.wa[:, 0:16], T.wi[:], 223, None, A.bitwise_and, None, wik, ["wa0"])
        ts(T.wa[:, 16:32], T.wi[:], 16, None, A.bitwise_and, None, wik, ["wa1"])
        ts(T.wa[:, 32:48], T.wi[:], 1, 16, A.logical_shift_right, A.bitwise_and, wik, ["wa2"])
        if t == R - 1:
            ts(T.wa[:, 48:64], T.wi[:], 255, None, A.bitwise_and, None, wik, ["wa3"])
        tt(T.tin[:, 0:16], T.wa[:, 0:16], T.wa[:, 16:32], A.add, ["wa0", "wa1"], ["tin0"])
        copy("v", T.tin[:, 32:48], T.wa[:, 32:48], ["wa2"], ["tin1"])
        if t == R - 1:
            copy("v", T.lown[:], T.wa[:, 48:64], ["wa3"], ["lown"])
            copy("s", T.lof[:], T.col[:].indirect(T.lown[:]), ["lown", "col"], ["lof"])
            dma("y", T.lo[:], T.lof[0:128:16, :], ["lof"], ["lo"])
        turn(T.y1[:], T.tin[:], ["tin0", "tin1", ("tinz", 0), ("tinz", 1)], ["y1"])
        for i in range(2):
            tt(T.y2[:, 16 * i:16 * i + 16], T.y1[:, 16 - 16 * i:32 - 16 * i], T.y1[:, 48 - 16 * i:64 - 16 * i], A.add, ["y1"], [("y2", i)])
        turn(T.y3[:], T.y2[:], [("y2", 0), ("y2", 1)], ["y3"])
        copy("v", T.lsib[:], T.y3[:, 0:16], ["y3"], ["lsib"])

    for t in range(R):
        for step in (state, places, send):
            for h in range(2):
                step(t, h)
        if t == 0:
            quant(T.qv[:], T.sv[:], T.vt[:], ["vt"], ["qv"])
        sibling(t)
        for h in range(2):
            layer(t, h)
        phase[0] += 1

    qx, sx = T["qx%d" % R], T["sx%d" % R]
    for h in range(2):
        state(R, h)
        dma("y", half(T.oc, h, w=512), u8(half(qx, h)), [("qx", R, h)], [("oc", h)])
        copy("v", half(T.yo, h), bank(h), [], [("ps", h), ("yo", h)])
        dma("sy"[h], half(T.y, h), half(T.yo, h), [("yo", h)], [("y", h)])
    for k in range(4):
        dma("sy"[k % 2], T.osc[4 * k:4 * k + 4, :], sx[32 * k:32 * k + 4, :], [("qx", R, 0), ("qx", R, 1)], [("osc", k)])

    count, wrote, readers = {}, {}, {}
    known = {q: {} for q in Q}

    def wait(q, tok):
        sem, c, snap = tok
        k = known[q]
        if k.get(sem, 0) >= c:
            return
        Q[q].wait_ge(T.sem[sem], c)
        k[sem] = c
        for s2, c2 in snap.items():
            if k.get(s2, 0) < c2:
                k[s2] = c2

    ndma = 0
    for c in in_order(calls):
        q = c["q"]
        deps = [wrote[k] for k in c["rd"] + c["wr"] if k in wrote] + [tk for k in c["wr"] for tk in readers.get(k, [])]
        for tk in sorted(deps, key=lambda tk: -tk[1]):
            wait(q, tk)
        if c["kind"] == "arrive":
            count[c["args"][0]] = c["args"][1]
            wait(q, c["args"] + ({},))
            continue
        made = c["fn"](*c["args"], **c["kw"])
        if c["kind"] == "remote":
            count["sent"] = count.get("sent", 0) + ones(mymask)
            continue
        sem, inc = ("d%d" % ndma, 16) if c["kind"] == "dma" else ("c" + q, 1)
        ndma += c["kind"] == "dma"
        made.then_inc(T.sem[sem], inc)
        count[sem] = count.get(sem, 0) + inc
        tok = (sem, count[sem], dict(known[q]))
        for k in c["rd"]:
            readers.setdefault(k, []).append(tok)
        for k in c["wr"]:
            wrote[k], readers[k] = tok, []
    for sem in sorted(count, key=lambda k: (k[0] == "d", len(k), k)):
        if not any(known[q].get(sem, 0) >= count[sem] for q in Q):
            wait("g", (sem, count[sem], {}))
